import numpy as np
import ml_dtypes


def mxq(x, axis, fmt="e4m3"):
    dtype, down = {"e4m3": (ml_dtypes.float8_e4m3fn, 7), "e5m2": (ml_dtypes.float8_e5m2, 14)}[fmt]
    v = np.moveaxis(np.asarray(x, np.float32).astype(ml_dtypes.bfloat16).astype(np.float64), axis, -1)
    blocks = v.reshape(v.shape[:-1] + (-1, 32))
    amax = np.abs(blocks).max(-1, keepdims=True)
    byte = np.maximum(np.where(amax > 0, np.frexp(amax)[1] - 1 + 127, 0) - down, 1)
    scale = np.exp2(byte - 127.0)
    codes = (blocks / scale).astype(np.float32).astype(dtype).astype(np.float64)
    return np.moveaxis((codes * scale).reshape(v.shape), -1, axis)


WIDE = False


def mx_kscale(k):
    if not WIDE:
        return np.ones(k)
    levels = np.array([10, -10, 5, -5, 0])
    if k % 512:
        return np.exp2(np.random.permutation(np.resize(levels, k // 32))).repeat(32)
    a = np.empty((k // 512, 16))
    for p in range(k // 512):
        a[p, :8] = np.random.permutation(np.resize(levels, 8))
        for g in range(8):
            far = levels[np.abs(levels - a[p, g]) >= 10]
            a[p, g + 8] = far[np.random.randint(len(far))]
    return np.exp2(a.ravel()).repeat(32)


def f64(x):
    return np.asarray(x).astype(np.float64)


def striped(idx):
    return np.tile(idx.reshape(-1, 16).T, (8, 1)).astype(np.uint16)


def unstriped(offs):
    return offs[:16].T.reshape(-1).astype(np.int64)


E2M1 = np.array([0.0, 0.5, 1.0, 1.5, 2.0, 3.0, 4.0, 6.0, -0.0, -0.5, -1.0, -1.5, -2.0, -3.0, -4.0, -6.0])


def pack_weight(w, fmt):
    k, n = w.shape
    w = f64(np.asarray(w, np.float32).astype(ml_dtypes.bfloat16)).reshape(k // 32, 32, n)
    amax = np.abs(w).max(1)
    if fmt == "e4m3":
        byte = np.frexp(amax)[1] - 1 + 127 - 7
    else:
        mant, ex = np.frexp(amax / 6.0)
        byte = np.where(mant > 0.5, ex, ex - 1) + 127
    byte = np.clip(np.where(amax > 0, byte, 1), 1, 254)
    scaled = (w * np.exp2(127.0 - byte)[:, None, :]).reshape(k, n).astype(np.float32)
    by_word = np.ascontiguousarray(scaled.reshape(k // 512, 128, 4, n).transpose(0, 1, 3, 2))
    if fmt == "e4m3":
        words = by_word.astype(ml_dtypes.float8_e4m3fn).view(np.uint8)
    else:
        c = by_word.astype(ml_dtypes.float4_e2m1fn).view(np.uint8) & 0xF
        words = (c[..., 0::2] | (c[..., 1::2] << 4)).reshape(k // 512, 128, 2 * n)
    return np.ascontiguousarray(words), np.ascontiguousarray(byte.astype(np.uint8).reshape(k // 512, 16, n))


def unpack_weight(words, scales, fmt):
    g, _, n = scales.shape
    words = np.ascontiguousarray(words).reshape(g, 128, n, -1)
    if fmt == "e4m3":
        vals = words.view(ml_dtypes.float8_e4m3fn).astype(np.float64)
    else:
        nib = np.empty((g, 128, n, 4), np.uint8)
        nib[..., 0::2] = words & 0xF
        nib[..., 1::2] = words >> 4
        vals = E2M1[nib]
    vals = vals * np.repeat(np.exp2(scales.astype(np.float64) - 127.0), 8, axis=1)[..., None]
    return vals.transpose(0, 1, 3, 2).reshape(g * 512, n)


def relu2(v):
    return np.maximum(v, 0.0) ** 2


K, T, E, C, H, TOP, COPIES = 1024, 512, 6, 128, 512, 2, 128
PAD = 64


def by_expert(wq, xq):
    return np.concatenate([wq[e].T @ xq[:, e * C:(e + 1) * C] for e in range(E)], axis=1)


def setup_inputs():
    n = np.random.standard_normal
    s = mx_kscale(K)
    u = mx_kscale(H)
    left = TOP * T - E * C - COPIES
    deal = np.repeat(np.arange(E + 2), [C] * E + [COPIES, left]).reshape(TOP, T)[:, np.random.permutation(T)]
    deal = np.take_along_axis(deal, np.argsort(np.random.rand(TOP, T), axis=0), axis=0)
    for _ in range(8):
        s_, t_ = np.random.permutation(T).reshape(2, -1); r = np.random.randint(TOP, size=T // 2); x, y = deal[r, s_].copy(), deal[r, t_].copy()
        ok = ~((deal[:, s_] == y).any(0) | (deal[:, t_] == x).any(0)); deal[r[ok], s_[ok]] = y[ok]; deal[r[ok], t_[ok]] = x[ok]
    order = np.lexsort((np.random.rand(TOP * T), deal.reshape(-1)))[:E * C]
    slot_token = order % T
    pos = np.where(deal == E, E * C + np.arange(T), E * C + T + np.arange(T) % PAD).reshape(-1); pos[order] = np.arange(E * C); pos = pos.reshape(TOP, T)
    g = np.random.uniform(0.5, 1.5, (TOP, T)); g = g / g.sum(0)
    xf = n((K, T))
    x = pack_weight(xf * s[:, None], "e4m3")
    w1 = [pack_weight(m, "e2m1") for m in n((E, K, H)) / np.sqrt(K) / s[None, :, None] * u]
    w2 = [pack_weight(m, "e2m1") for m in n((E, H, K)) / np.sqrt(H) / u[None, :, None] ** 2]
    return {
        "x_words": x[0],
        "x_scales": x[1],
        "xr": (xf).astype(np.float32),
        "w1_words": np.stack([m[0] for m in w1]),
        "w1_scales": np.stack([m[1] for m in w1]),
        "w2_words": np.stack([m[0] for m in w2]),
        "w2_scales": np.stack([m[1] for m in w2]),
        "gate": np.stack([np.tile(r, (128, 1)) for r in g]).astype(np.float32),
        "offs": striped(slot_token),
        "pos1": striped(pos[0]),
        "pos2": striped(pos[1]),
    }


def reference(x_words, x_scales, xr, w1_words, w1_scales, w2_words, w2_scales, gate, offs, pos1, pos2):
    w1 = np.stack([unpack_weight(w1_words[e], w1_scales[e], "e2m1") for e in range(E)])
    w2 = np.stack([unpack_weight(w2_words[e], w2_scales[e], "e2m1") for e in range(E)])
    idx = unstriped(offs)
    xq = unpack_weight(x_words, x_scales, "e4m3")[:, idx]
    h = relu2(by_expert(w1, xq))
    y = by_expert(w2, mxq(h, 0, "e4m3"))
    y = np.concatenate([y, f64(xr), np.zeros((K, PAD))], axis=1)
    out = sum(f64(gate[r, :1]) * y[:, unstriped(p)] for r, p in enumerate((pos1, pos2)))
    return out

@@ -1,0 +1,178 @@
+from contextlib import ExitStack
+
+import concourse.mybir as mybir
+from concourse.masks import make_identity
+
+K, T, E, C, H, PAD = 1024, 512, 6, 128, 512, 64
+FLOPS = 2 * 2 * E * C * K * H
+
+F32 = mybir.dt.float32
+BF16 = mybir.dt.bfloat16
+I32 = mybir.dt.int32
+U32 = mybir.dt.uint32
+U16 = mybir.dt.uint16
+U8 = mybir.dt.uint8
+FP8X4 = mybir.dt.float8_e4m3fn_x4
+FP4X4 = mybir.dt.float4_e2m1fn_x4
+ACT = mybir.ActivationFunctionType
+ALU = mybir.AluOpType
+
+P = 128
+PACK = 4
+PASSES = K // (P * PACK)
+SLOTS = E * C
+BLOCKS = K // P
+WINDOW = SLOTS + T + PAD
+BANK = 512
+GATHER_EXPERTS = [(0, 1), (1, 3), (3, 5), (5, 6)]
+
+
+def tile_moe_cpy_mlp_relu2_kernel(
+    tc, x_words, x_scales, xr, w1_words, w1_scales, w2_words, w2_scales, gate, offs, pos1, pos2, out
+):
+    nc = tc.nc
+    with ExitStack() as ctx:
+        keep = ctx.enter_context(tc.tile_pool(name="keep", bufs=1))
+        ring = ctx.enter_context(tc.tile_pool(name="ring", bufs=3))
+        psum = ctx.enter_context(tc.psum_pool(name="psum", bufs=2))
+
+        offs_sb = keep.tile([P, SLOTS // 16], U16, name="offs_sb")
+        pos1_sb = keep.tile([P, T // 16], U16, name="pos1_sb")
+        pos2_sb = keep.tile([P, T // 16], U16, name="pos2_sb")
+        xw = [keep.tile([P, T], I32, name=f"xw{s}", align_bytes=64) for s in range(PASSES)]
+        xs = keep.tile([P, PASSES, T // 4], I32, name="xs", align_bytes=64)
+        w1 = [keep.tile([P, PASSES, 2 * H], U8, name=f"w1_{e}", align_bytes=64) for e in range(E)]
+        w1s = keep.tile([P, E * PASSES, H // 4], I32, name="w1s", align_bytes=64)
+        w2 = [keep.tile([P, E, K], U8, name=f"w2_{hf}", align_bytes=64) for hf in range(2)]
+        w2s = keep.tile([P, E, K // 4], I32, name="w2s", align_bytes=64)
+        gates = [keep.tile([P, T], F32, name=f"gate{r}") for r in range(2)]
+        win = [keep.tile([P, WINDOW], F32, name=f"win{b}") for b in range(BLOCKS)]
+        ident = keep.tile([P, P], F32, name="ident")
+        zeros = keep.tile([P, PAD], F32, name="zeros")
+        xg = [keep.tile([P, SLOTS], U32, name=f"xg{s}", align_bytes=64) for s in range(PASSES)]
+        sg = [keep.tile([P, SLOTS], U8, name=f"sg{s}", align_bytes=64) for s in range(PASSES)]
+        hq = keep.tile([P, SLOTS], U32, name="hq", align_bytes=64)
+        hs = keep.tile([P, SLOTS], U8, name="hs", align_bytes=64)
+        hb = keep.tile([P, SLOTS, PACK], BF16, name="hb", align_bytes=64)
+
+        nc.gpsimd.memset(w1s[:, :E, :], 0)
+        nc.vector.memset(xs[:], 0)
+        nc.vector.memset(w1s[:, E:, :], 0)
+        nc.vector.memset(w2s[:], 0)
+        nc.gpsimd.memset(zeros[:], 0.0)
+        make_identity(nc, ident[:])
+        for b in range(BLOCKS):
+            nc.scalar.activation(win[b][:, SLOTS + T :], zeros[:], ACT.Copy)
+
+        def load_scales(plane, rows):
+            for r in range(4):
+                nc.sync.dma_start(plane[r:P:32, :, :], rows[r].bitcast(I32))
+
+        def load_xr(b):
+            nc.sync.dma_start(win[b][:, SLOTS : SLOTS + T], xr[b * P : (b + 1) * P, :])
+
+        def load_w1(e):
+            nc.sync.dma_start(w1[e][:].bitcast(I32), w1_words[e].rearrange("s p c -> p s c").bitcast(I32))
+
+        def load_w2(hf):
+            src = w2_words.rearrange("e o p c -> p (e o) c")[:, :, hf * K : (hf + 1) * K]
+            nc.sync.dma_start(w2[hf][:].bitcast(I32), src.bitcast(I32))
+
+        nc.sync.dma_start(offs_sb[:], offs)
+        for s in range(PASSES):
+            nc.sync.dma_start(xw[s][:], x_words[s].rearrange("p t d -> p (t d)").bitcast(I32))
+        load_scales(xs, x_scales.rearrange("s (q r) t -> r q s t", r=4))
+        load_w1(0)
+        load_scales(w1s, w1_scales.rearrange("e s (q r) i -> r q (e s) i", r=4))
+        for e in range(1, E):
+            load_w1(e)
+        load_scales(w2s, w2_scales.rearrange("e o (q r) n -> r q (e o) n", r=4))
+        load_w2(0)
+        nc.sync.dma_start(pos1_sb[:], pos1)
+        nc.sync.dma_start(pos2_sb[:], pos2)
+        nc.sync.dma_start(gates[0][:], gate[0])
+        load_xr(0)
+        nc.sync.dma_start(gates[1][:], gate[1])
+        load_xr(1)
+        load_xr(2)
+        load_w2(1)
+        for b in range(3, BLOCKS):
+            load_xr(b)
+
+        for e0, e1 in GATHER_EXPERTS:
+            cols = slice(e0 * C, e1 * C)
+            idx = offs_sb[:, e0 * C // 16 : e1 * C // 16]
+            for s in range(PASSES):
+                nc.vector.tensor_copy(xg[s][:, cols], xw[s][:].bitcast(U32).indirect(idx))
+                nc.vector.tensor_copy(sg[s][:, cols], xs[:, s, :].bitcast(U8).indirect(idx))
+
+        for e in range(E):
+            cols = slice(e * C, (e + 1) * C)
+            pre = psum.tile([P, H], F32, name="pre")
+            for s in range(PASSES):
+                nc.tensor.matmul_mx(
+                    out=pre[:],
+                    lhsT=xg[s][:, cols].bitcast(FP8X4),
+                    lhsT_scale=sg[s][:, cols],
+                    rhs=w1[e][:, s, :].bitcast(FP4X4),
+                    rhs_scale=w1s[:, e * PASSES + s, :].bitcast(U8),
+                    start=(s == 0),
+                    stop=(s == PASSES - 1),
+                )
+            pos = ring.tile([P, PACK, P], F32, name="pos")
+            by_plane = pre[:].rearrange("p (m j) -> p j m", j=PACK)
+            if e == E - 1:
+                nc.vector.tensor_scalar_max(pos[:], by_plane, 0.0)
+            else:
+                nc.scalar.activation(pos[:], by_plane, ACT.Relu)
+            turned = psum.tile([P, PACK, C], F32, name="turned")
+            for j in range(PACK):
+                nc.tensor.transpose(turned[:, j, :], pos[:, j, :], ident[:])
+            nc.scalar.activation(hb[:, cols, :], turned[:].rearrange("p j u -> p u j"), ACT.Square)
+            if e >= 3:
+                done = slice(0 if e == 3 else e * C, (e + 1) * C)
+                nc.vector.quantize_mx(
+                    out=hq[:, done].bitcast(FP8X4),
+                    scales=hs[:, done],
+                    in_=hb[:, done, :].rearrange("p u j -> p (u j)"),
+                )
+
+        def second_layer(b):
+            hf, c0 = divmod(b * P, K // 2)
+            for name, e0, e1 in (("ya", 0, 4), ("yb", 4, E)):
+                y = psum.tile([P, (e1 - e0) * C], F32, name=name)
+                for e in range(e0, e1):
+                    cols = slice(e * C, (e + 1) * C)
+                    nc.tensor.matmul_mx(
+                        out=y[:, (e - e0) * C : (e - e0 + 1) * C],
+                        lhsT=w2[hf][:, e, 2 * c0 : 2 * (c0 + P)].bitcast(FP4X4),
+                        lhsT_scale=w2s[:, e, b * P // 4 : (b + 1) * P // 4].bitcast(U8),
+                        rhs=hq[:, cols].bitcast(FP8X4),
+                        rhs_scale=hs[:, cols],
+                        start=True,
+                        stop=True,
+                    )
+                if b == 0:
+                    nc.vector.tensor_copy(win[b][:, e0 * C : e1 * C], y[:])
+                else:
+                    nc.scalar.activation(win[b][:, e0 * C : e1 * C], y[:], ACT.Copy)
+
+        def add_and_store(b, t0, t1, first, second):
+            res = ring.tile([P, t1 - t0], F32, name="res")
+            nc.vector.tensor_tensor(res[:], first[:], second[:], ALU.add)
+            nc.sync.dma_start(out[b * P : (b + 1) * P, t0:t1], res[:])
+
+        pieces = [(b, 0, T) for b in range(BLOCKS - 1)] + [(BLOCKS - 1, 0, T // 2), (BLOCKS - 1, T // 2, T)]
+        waiting = None
+        for b, t0, t1 in pieces:
+            if t0 == 0:
+                second_layer(b)
+            idx = slice(t0 // 16, t1 // 16)
+            first = ring.tile([P, t1 - t0], F32, name="first")
+            nc.vector.tensor_tensor(first[:], win[b][:].indirect(pos1_sb[:, idx]), gates[0][:, t0:t1], ALU.mult)
+            if waiting is not None:
+                add_and_store(*waiting)
+            second = ring.tile([P, t1 - t0], F32, name="second")
+            nc.vector.tensor_tensor(second[:], win[b][:].indirect(pos2_sb[:, idx]), gates[1][:, t0:t1], ALU.mult)
+            waiting = (b, t0, t1, first, second)
+        add_and_store(*waiting)

@@ -1,7 +1,6 @@
 from contextlib import ExitStack
 
 import concourse.mybir as mybir
-from concourse.masks import make_identity
 
 K, T, E, C, H, PAD = 1024, 512, 6, 128, 512, 64
 FLOPS = 2 * 2 * E * C * K * H
@@ -23,8 +22,10 @@ PASSES = K // (P * PACK)
 SLOTS = E * C
 BLOCKS = K // P
 WINDOW = SLOTS + T + PAD
-BANK = 512
+TENSOR_ADDS = 7
 GATHER_EXPERTS = [(0, 1), (1, 3), (3, 5), (5, 6)]
+W1_LOADS = [(0, 1), (1, 3), (3, 6)]
+VECTOR_RELU_FROM = 4
 
 
 def tile_moe_cpy_mlp_relu2_kernel(
@@ -34,108 +35,127 @@ def tile_moe_cpy_mlp_relu2_kernel(
     with ExitStack() as ctx:
         keep = ctx.enter_context(tc.tile_pool(name="keep", bufs=1))
         ring = ctx.enter_context(tc.tile_pool(name="ring", bufs=3))
+        prods = ctx.enter_context(tc.tile_pool(name="prods", bufs=5))
         psum = ctx.enter_context(tc.psum_pool(name="psum", bufs=2))
 
         offs_sb = keep.tile([P, SLOTS // 16], U16, name="offs_sb")
         pos1_sb = keep.tile([P, T // 16], U16, name="pos1_sb")
         pos2_sb = keep.tile([P, T // 16], U16, name="pos2_sb")
-        xw = [keep.tile([P, T], I32, name=f"xw{s}", align_bytes=64) for s in range(PASSES)]
+        xw = keep.tile([P, PASSES, T], I32, name="xw", align_bytes=64)
         xs = keep.tile([P, PASSES, T // 4], I32, name="xs", align_bytes=64)
-        w1 = [keep.tile([P, PASSES, 2 * H], U8, name=f"w1_{e}", align_bytes=64) for e in range(E)]
         w1s = keep.tile([P, E * PASSES, H // 4], I32, name="w1s", align_bytes=64)
-        w2 = [keep.tile([P, E, K], U8, name=f"w2_{hf}", align_bytes=64) for hf in range(2)]
-        w2s = keep.tile([P, E, K // 4], I32, name="w2s", align_bytes=64)
-        gates = [keep.tile([P, T], F32, name=f"gate{r}") for r in range(2)]
-        win = [keep.tile([P, WINDOW], F32, name=f"win{b}") for b in range(BLOCKS)]
         ident = keep.tile([P, P], F32, name="ident")
         zeros = keep.tile([P, PAD], F32, name="zeros")
-        xg = [keep.tile([P, SLOTS], U32, name=f"xg{s}", align_bytes=64) for s in range(PASSES)]
-        sg = [keep.tile([P, SLOTS], U8, name=f"sg{s}", align_bytes=64) for s in range(PASSES)]
+        w2s = keep.tile([P, E, K // 4], I32, name="w2s", align_bytes=64)
+        hb = keep.tile([P, SLOTS, PACK], BF16, name="hb", align_bytes=64)
         hq = keep.tile([P, SLOTS], U32, name="hq", align_bytes=64)
         hs = keep.tile([P, SLOTS], U8, name="hs", align_bytes=64)
-        hb = keep.tile([P, SLOTS, PACK], BF16, name="hb", align_bytes=64)
-
-        nc.gpsimd.memset(w1s[:, :E, :], 0)
-        nc.vector.memset(xs[:], 0)
-        nc.vector.memset(w1s[:, E:, :], 0)
-        nc.vector.memset(w2s[:], 0)
-        nc.gpsimd.memset(zeros[:], 0.0)
-        make_identity(nc, ident[:])
-        for b in range(BLOCKS):
-            nc.scalar.activation(win[b][:, SLOTS + T :], zeros[:], ACT.Copy)
 
         def load_scales(plane, rows):
             for r in range(4):
                 nc.sync.dma_start(plane[r:P:32, :, :], rows[r].bitcast(I32))
 
-        def load_xr(b):
-            nc.sync.dma_start(win[b][:, SLOTS : SLOTS + T], xr[b * P : (b + 1) * P, :])
-
-        def load_w1(e):
-            nc.sync.dma_start(w1[e][:].bitcast(I32), w1_words[e].rearrange("s p c -> p s c").bitcast(I32))
-
-        def load_w2(hf):
-            src = w2_words.rearrange("e o p c -> p (e o) c")[:, :, hf * K : (hf + 1) * K]
-            nc.sync.dma_start(w2[hf][:].bitcast(I32), src.bitcast(I32))
-
+        nc.gpsimd.memset(xs[:], 0)
+        nc.gpsimd.memset(zeros[:], 0.0)
+        nc.vector.memset(w1s[:], 0)
         nc.sync.dma_start(offs_sb[:], offs)
-        for s in range(PASSES):
-            nc.sync.dma_start(xw[s][:], x_words[s].rearrange("p t d -> p (t d)").bitcast(I32))
+        nc.sync.dma_start(xw[:], x_words.rearrange("s p t d -> p s (t d)").bitcast(I32))
         load_scales(xs, x_scales.rearrange("s (q r) t -> r q s t", r=4))
-        load_w1(0)
         load_scales(w1s, w1_scales.rearrange("e s (q r) i -> r q (e s) i", r=4))
-        for e in range(1, E):
-            load_w1(e)
-        load_scales(w2s, w2_scales.rearrange("e o (q r) n -> r q (e o) n", r=4))
-        load_w2(0)
         nc.sync.dma_start(pos1_sb[:], pos1)
         nc.sync.dma_start(pos2_sb[:], pos2)
-        nc.sync.dma_start(gates[0][:], gate[0])
-        load_xr(0)
-        nc.sync.dma_start(gates[1][:], gate[1])
-        load_xr(1)
-        load_xr(2)
-        load_w2(1)
-        for b in range(3, BLOCKS):
-            load_xr(b)
 
-        for e0, e1 in GATHER_EXPERTS:
-            cols = slice(e0 * C, e1 * C)
-            idx = offs_sb[:, e0 * C // 16 : e1 * C // 16]
-            for s in range(PASSES):
-                nc.vector.tensor_copy(xg[s][:, cols], xw[s][:].bitcast(U32).indirect(idx))
-                nc.vector.tensor_copy(sg[s][:, cols], xs[:, s, :].bitcast(U8).indirect(idx))
+        with tc.tile_pool(name="setup", bufs=1) as setup:
+            blank = setup.tile([P, P], F32, name="blank")
+            nc.vector.memset(blank[:], 0.0)
+            nc.gpsimd.affine_select(
+                out=ident[:],
+                in_=blank[:],
+                compare_op=ALU.not_equal,
+                fill=1.0,
+                base=0,
+                pattern=[[-1, P]],
+                channel_multiplier=1,
+            )
 
-        for e in range(E):
-            cols = slice(e * C, (e + 1) * C)
-            pre = psum.tile([P, H], F32, name="pre")
-            for s in range(PASSES):
-                nc.tensor.matmul_mx(
-                    out=pre[:],
-                    lhsT=xg[s][:, cols].bitcast(FP8X4),
-                    lhsT_scale=sg[s][:, cols],
-                    rhs=w1[e][:, s, :].bitcast(FP4X4),
-                    rhs_scale=w1s[:, e * PASSES + s, :].bitcast(U8),
-                    start=(s == 0),
-                    stop=(s == PASSES - 1),
-                )
-            pos = ring.tile([P, PACK, P], F32, name="pos")
-            by_plane = pre[:].rearrange("p (m j) -> p j m", j=PACK)
-            if e == E - 1:
-                nc.vector.tensor_scalar_max(pos[:], by_plane, 0.0)
-            else:
-                nc.scalar.activation(pos[:], by_plane, ACT.Relu)
-            turned = psum.tile([P, PACK, C], F32, name="turned")
-            for j in range(PACK):
-                nc.tensor.transpose(turned[:, j, :], pos[:, j, :], ident[:])
-            nc.scalar.activation(hb[:, cols, :], turned[:].rearrange("p j u -> p u j"), ACT.Square)
-            if e >= 3:
-                done = slice(0 if e == 3 else e * C, (e + 1) * C)
-                nc.vector.quantize_mx(
-                    out=hq[:, done].bitcast(FP8X4),
-                    scales=hs[:, done],
-                    in_=hb[:, done, :].rearrange("p u j -> p (u j)"),
-                )
+        big = ctx.enter_context(tc.tile_pool(name="big", bufs=1))
+
+        def load_xr(win, b):
+            nc.sync.dma_start(win[:, SLOTS : SLOTS + T], xr[b * P : (b + 1) * P, :])
+
+        def load_w2(tile, hf):
+            src = w2_words.rearrange("e o p c -> p (e o) c")[:, :, hf * K : (hf + 1) * K]
+            nc.sync.dma_start(tile[:].bitcast(I32), src.bitcast(I32))
+
+        w1 = []
+        for n, (e0, e1) in enumerate(W1_LOADS):
+            tile = big.tile([P, (e1 - e0) * PASSES, 2 * H], U8, name=f"w1_{n}", tag=f"slot{n}", align_bytes=64)
+            nc.sync.dma_start(tile[:].bitcast(I32), w1_words[e0:e1].rearrange("e s p c -> p (e s) c").bitcast(I32))
+            w1 += [tile[:, (e - e0) * PASSES : (e - e0 + 1) * PASSES, :] for e in range(e0, e1)]
+        nc.vector.memset(w2s[:], 0)
+        load_scales(w2s, w2_scales.rearrange("e o (q r) n -> r q (e o) n", r=4))
+        wins = [big.tile([P, WINDOW], F32, name="win0")]
+        load_xr(wins[0], 0)
+        nc.scalar.activation(wins[0][:, SLOTS + T :], zeros[:], ACT.Copy)
+
+        with tc.tile_pool(name="gathered", bufs=2, side="right") as gathered:
+            tokens = []
+            for e0, e1 in GATHER_EXPERTS:
+                width = (e1 - e0) * C
+                idx = offs_sb[:, e0 * C // 16 : e1 * C // 16]
+                xg = [gathered.tile([P, width], U32, name=f"xg{s}", align_bytes=64) for s in range(PASSES)]
+                sg = [gathered.tile([P, width], U8, name=f"sg{s}", align_bytes=64) for s in range(PASSES)]
+                for s in range(PASSES):
+                    nc.vector.tensor_copy(xg[s][:], xw[:, s, :].bitcast(U32).indirect(idx))
+                for s in range(PASSES):
+                    nc.vector.tensor_copy(sg[s][:], xs[:, s, :].bitcast(U8).indirect(idx))
+                tokens += [(xg, sg, slice((e - e0) * C, (e - e0 + 1) * C)) for e in range(e0, e1)]
+
+            for e in range(E):
+                cols = slice(e * C, (e + 1) * C)
+                xg, sg, own = tokens[e]
+                pre = psum.tile([P, H], F32, name="pre")
+                for s in range(PASSES):
+                    nc.tensor.matmul_mx(
+                        out=pre[:],
+                        lhsT=xg[s][:, own].bitcast(FP8X4),
+                        lhsT_scale=sg[s][:, own],
+                        rhs=w1[e][:, s, :].bitcast(FP4X4),
+                        rhs_scale=w1s[:, e * PASSES + s, :].bitcast(U8),
+                        start=(s == 0),
+                        stop=(s == PASSES - 1),
+                    )
+                pos = ring.tile([P, PACK, P], F32, name="pos")
+                by_plane = pre[:].rearrange("p (m j) -> p j m", j=PACK)
+                if e >= VECTOR_RELU_FROM:
+                    nc.vector.tensor_scalar_max(pos[:], by_plane, 0.0)
+                else:
+                    nc.scalar.activation(pos[:], by_plane, ACT.Relu)
+                turned = psum.tile([P, PACK, C], F32, name="turned")
+                for j in range(PACK):
+                    nc.tensor.transpose(turned[:, j, :], pos[:, j, :], ident[:])
+                nc.scalar.activation(hb[:, cols, :], turned[:].rearrange("p j u -> p u j"), ACT.Square)
+
+        w2 = [big.tile([P, E, K], U8, name="w2_0", tag="slot0", align_bytes=64)]
+        load_w2(w2[0], 0)
+        gates = big.tile([P, 2, T], F32, name="gates", tag="slot1", align_bytes=64)
+        nc.sync.dma_start(gates[:], gate.rearrange("r p t -> p r t"))
+        late = ctx.enter_context(tc.tile_pool(name="late", bufs=1, side="right"))
+        for b in range(1, BLOCKS):
+            wins.append(late.tile([P, WINDOW], F32, name=f"win{b}"))
+            load_xr(wins[b], b)
+            nc.gpsimd.memset(wins[b][:, SLOTS + T :], 0.0)
+            if b == 3:
+                w2.append(late.tile([P, E, K], U8, name="w2_1", align_bytes=64))
+                load_w2(w2[1], 1)
+
+        for e0, e1 in ((0, 4), (4, 5), (5, 6)):
+            done = slice(e0 * C, e1 * C)
+            nc.vector.quantize_mx(
+                out=hq[:, done].bitcast(FP8X4),
+                scales=hs[:, done],
+                in_=hb[:, done, :].rearrange("p u j -> p (u j)"),
+            )
 
         def second_layer(b):
             hf, c0 = divmod(b * P, K // 2)
@@ -153,26 +173,48 @@ def tile_moe_cpy_mlp_relu2_kernel(
                         stop=True,
                     )
                 if b == 0:
-                    nc.vector.tensor_copy(win[b][:, e0 * C : e1 * C], y[:])
+                    nc.vector.tensor_copy(wins[b][:, e0 * C : e1 * C], y[:])
                 else:
-                    nc.scalar.activation(win[b][:, e0 * C : e1 * C], y[:], ACT.Copy)
+                    nc.scalar.activation(wins[b][:, e0 * C : e1 * C], y[:], ACT.Copy)
 
         def add_and_store(b, t0, t1, first, second):
             res = ring.tile([P, t1 - t0], F32, name="res")
-            nc.vector.tensor_tensor(res[:], first[:], second[:], ALU.add)
+            if b < TENSOR_ADDS:
+                total = psum.tile([P, T // P, P], F32, name="pre")
+                for q in range(T // P):
+                    for term, opens in ((first, True), (second, False)):
+                        nc.tensor.matmul(
+                            total[:, q, :],
+                            term[:, q * P : (q + 1) * P],
+                            ident[:],
+                            start=opens,
+                            stop=not opens,
+                            is_transpose=True,
+                        )
+                total_sb = ring.tile([P, T // P, P], F32, name="pos")
+                nc.scalar.activation(total_sb[:], total[:], ACT.Copy)
+                back = psum.tile([P, T // P, P], F32, name="turned")
+                for q in range(T // P):
+                    nc.tensor.transpose(back[:, q, :], total_sb[:, q, :], ident[:])
+                nc.scalar.activation(res[:], back[:].rearrange("p q t -> p (q t)"), ACT.Copy)
+            else:
+                nc.vector.tensor_tensor(res[:], first[:], second[:], ALU.add)
             nc.sync.dma_start(out[b * P : (b + 1) * P, t0:t1], res[:])
+
+        second_layer(0)
+        second_layer(1)
 
         pieces = [(b, 0, T) for b in range(BLOCKS - 1)] + [(BLOCKS - 1, 0, T // 2), (BLOCKS - 1, T // 2, T)]
         waiting = None
         for b, t0, t1 in pieces:
-            if t0 == 0:
-                second_layer(b)
+            if t0 == 0 and b + 2 < BLOCKS:
+                second_layer(b + 2)
             idx = slice(t0 // 16, t1 // 16)
-            first = ring.tile([P, t1 - t0], F32, name="first")
-            nc.vector.tensor_tensor(first[:], win[b][:].indirect(pos1_sb[:, idx]), gates[0][:, t0:t1], ALU.mult)
+            first = prods.tile([P, t1 - t0], F32, name="first")
+            nc.vector.tensor_tensor(first[:], wins[b][:].indirect(pos1_sb[:, idx]), gates[:, 0, t0:t1], ALU.mult)
             if waiting is not None:
                 add_and_store(*waiting)
-            second = ring.tile([P, t1 - t0], F32, name="second")
-            nc.vector.tensor_tensor(second[:], win[b][:].indirect(pos2_sb[:, idx]), gates[1][:, t0:t1], ALU.mult)
+            second = prods.tile([P, t1 - t0], F32, name="second")
+            nc.vector.tensor_tensor(second[:], wins[b][:].indirect(pos2_sb[:, idx]), gates[:, 1, t0:t1], ALU.mult)
             waiting = (b, t0, t1, first, second)
         add_and_store(*waiting)

@@ -59,7 +59,8 @@ def tile_moe_cpy_mlp_relu2_kernel(
         nc.gpsimd.memset(zeros[:], 0.0)
         nc.vector.memset(w1s[:], 0)
         nc.sync.dma_start(offs_sb[:], offs)
-        nc.sync.dma_start(xw[:], x_words.rearrange("s p t d -> p s (t d)").bitcast(I32))
+        for s in range(PASSES):
+            nc.sync.dma_start(xw[:, s, :], x_words[s].rearrange("p t d -> p (t d)").bitcast(I32))
         load_scales(xs, x_scales.rearrange("s (q r) t -> r q s t", r=4))
         load_scales(w1s, w1_scales.rearrange("e s (q r) i -> r q (e s) i", r=4))
         nc.sync.dma_start(pos1_sb[:], pos1)
@@ -104,7 +105,7 @@ def tile_moe_cpy_mlp_relu2_kernel(
                 width = (e1 - e0) * C
                 idx = offs_sb[:, e0 * C // 16 : e1 * C // 16]
                 xg = [gathered.tile([P, width], U32, name=f"xg{s}", align_bytes=64) for s in range(PASSES)]
-                sg = [gathered.tile([P, width], U8, name=f"sg{s}", align_bytes=64) for s in range(PASSES)]
+                sg = [gathered.tile([P, width], U8, name=f"sg{s}", align_bytes=64, bufs=4) for s in range(PASSES)]
                 for s in range(PASSES):
                     nc.vector.tensor_copy(xg[s][:], xw[:, s, :].bitcast(U32).indirect(idx))
                 for s in range(PASSES):
@@ -114,7 +115,7 @@ def tile_moe_cpy_mlp_relu2_kernel(
             for e in range(E):
                 cols = slice(e * C, (e + 1) * C)
                 xg, sg, own = tokens[e]
-                pre = psum.tile([P, H], F32, name="pre")
+                pre = psum.tile([P, H], F32, name="pre", bufs=3)
                 for s in range(PASSES):
                     nc.tensor.matmul_mx(
                         out=pre[:],
@@ -159,8 +160,8 @@ def tile_moe_cpy_mlp_relu2_kernel(
 
         def second_layer(b):
             hf, c0 = divmod(b * P, K // 2)
-            for name, e0, e1 in (("ya", 0, 4), ("yb", 4, E)):
-                y = psum.tile([P, (e1 - e0) * C], F32, name=name)
+            for name, e0, e1, depth in (("ya", 0, 4, 2), ("yb", 4, E, 1)):
+                y = psum.tile([P, (e1 - e0) * C], F32, name=name, bufs=depth)
                 for e in range(e0, e1):
                     cols = slice(e * C, (e + 1) * C)
                     nc.tensor.matmul_mx(
@@ -178,17 +179,17 @@ def tile_moe_cpy_mlp_relu2_kernel(
                     nc.scalar.activation(wins[b][:, e0 * C : e1 * C], y[:], ACT.Copy)
 
         def add_and_store(b, t0, t1, first, second):
-            res = ring.tile([P, t1 - t0], F32, name="res")
+            res = ring.tile([P, t1 - t0], F32, name="res", bufs=BLOCKS + 1)
             if b < TENSOR_ADDS:
-                total = psum.tile([P, T // P, P], F32, name="pre")
-                for q in range(T // P):
-                    for term, opens in ((first, True), (second, False)):
+                total = psum.tile([P, T // P, P], F32, name="pre", bufs=3)
+                for r, term in enumerate((first, second)):
+                    for q in range(T // P):
                         nc.tensor.matmul(
                             total[:, q, :],
                             term[:, q * P : (q + 1) * P],
                             ident[:],
-                            start=opens,
-                            stop=not opens,
+                            start=(r == 0 and q == 0),
+                            stop=(r == 1 and q == T // P - 1),
                             is_transpose=True,
                         )
                 total_sb = ring.tile([P, T // P, P], F32, name="pos")

@@ -22,10 +22,10 @@ PASSES = K // (P * PACK)
 SLOTS = E * C
 BLOCKS = K // P
 WINDOW = SLOTS + T + PAD
-TENSOR_ADDS = 7
+TENSOR_ADDS = 6
 GATHER_EXPERTS = [(0, 1), (1, 3), (3, 5), (5, 6)]
 W1_LOADS = [(0, 1), (1, 3), (3, 6)]
-VECTOR_RELU_FROM = 4
+VECTOR_RELU_FROM = 3
 
 
 def tile_moe_cpy_mlp_relu2_kernel(
@@ -35,7 +35,7 @@ def tile_moe_cpy_mlp_relu2_kernel(
     with ExitStack() as ctx:
         keep = ctx.enter_context(tc.tile_pool(name="keep", bufs=1))
         ring = ctx.enter_context(tc.tile_pool(name="ring", bufs=3))
-        prods = ctx.enter_context(tc.tile_pool(name="prods", bufs=5))
+        prods = ctx.enter_context(tc.tile_pool(name="prods", bufs=8))
         psum = ctx.enter_context(tc.psum_pool(name="psum", bufs=2))
 
         offs_sb = keep.tile([P, SLOTS // 16], U16, name="offs_sb")
@@ -105,15 +105,15 @@ def tile_moe_cpy_mlp_relu2_kernel(
                 width = (e1 - e0) * C
                 idx = offs_sb[:, e0 * C // 16 : e1 * C // 16]
                 xg = [gathered.tile([P, width], U32, name=f"xg{s}", align_bytes=64) for s in range(PASSES)]
-                sg = [gathered.tile([P, width], U8, name=f"sg{s}", align_bytes=64, bufs=4) for s in range(PASSES)]
+                sg = [gathered.tile([P, width], U8, name=f"sg{s}", align_bytes=64, bufs=3) for s in range(PASSES)]
                 for s in range(PASSES):
                     nc.vector.tensor_copy(xg[s][:], xw[:, s, :].bitcast(U32).indirect(idx))
                 for s in range(PASSES):
                     nc.vector.tensor_copy(sg[s][:], xs[:, s, :].bitcast(U8).indirect(idx))
                 tokens += [(xg, sg, slice((e - e0) * C, (e - e0 + 1) * C)) for e in range(e0, e1)]
 
+            positive = []
             for e in range(E):
-                cols = slice(e * C, (e + 1) * C)
                 xg, sg, own = tokens[e]
                 pre = psum.tile([P, H], F32, name="pre", bufs=3)
                 for s in range(PASSES):
@@ -126,16 +126,26 @@ def tile_moe_cpy_mlp_relu2_kernel(
                         start=(s == 0),
                         stop=(s == PASSES - 1),
                     )
-                pos = ring.tile([P, PACK, P], F32, name="pos")
-                by_plane = pre[:].rearrange("p (m j) -> p j m", j=PACK)
+                pos = ring.tile([P, 2, P, 2], F32, name="pos", bufs=E)
+                positive.append(pos)
+                by_pair = pre[:].rearrange("p (m u c) -> p u m c", u=2, c=2)
                 if e >= VECTOR_RELU_FROM:
-                    nc.vector.tensor_scalar_max(pos[:], by_plane, 0.0)
+                    nc.vector.tensor_scalar_max(pos[:], by_pair, 0.0)
                 else:
-                    nc.scalar.activation(pos[:], by_plane, ACT.Relu)
-                turned = psum.tile([P, PACK, C], F32, name="turned")
-                for j in range(PACK):
-                    nc.tensor.transpose(turned[:, j, :], pos[:, j, :], ident[:])
-                nc.scalar.activation(hb[:, cols, :], turned[:].rearrange("p j u -> p u j"), ACT.Square)
+                    nc.scalar.activation(pos[:], by_pair, ACT.Relu)
+
+        for e, pos in enumerate(positive):
+            cols = slice(e * C, (e + 1) * C)
+            h = ring.tile([P, 2, 2 * P], BF16, name="h")
+            nc.scalar.activation(h[:], pos[:].rearrange("p u m c -> p u (m c)"), ACT.Square)
+            turned = psum.tile([P, 2, C], F32, name="turned")
+            for u in range(2):
+                nc.tensor.transpose(turned[:, u, :], h[:, u, :].bitcast(F32), ident[:])
+            pairs = hb[:, cols, :].bitcast(F32)
+            if e >= VECTOR_RELU_FROM:
+                nc.vector.tensor_copy(pairs, turned[:].rearrange("p u s -> p s u"))
+            else:
+                nc.scalar.copy(pairs, turned[:].rearrange("p u s -> p s u"))
 
         w2 = [big.tile([P, E, K], U8, name="w2_0", tag="slot0", align_bytes=64)]
         load_w2(w2[0], 0)
@@ -146,7 +156,7 @@ def tile_moe_cpy_mlp_relu2_kernel(
             wins.append(late.tile([P, WINDOW], F32, name=f"win{b}"))
             load_xr(wins[b], b)
             nc.gpsimd.memset(wins[b][:, SLOTS + T :], 0.0)
-            if b == 3:
+            if b == 1:
                 w2.append(late.tile([P, E, K], U8, name="w2_1", align_bytes=64))
                 load_w2(w2[1], 1)
 
@@ -173,7 +183,7 @@ def tile_moe_cpy_mlp_relu2_kernel(
                         start=True,
                         stop=True,
                     )
-                if b == 0:
+                if b == 0 and e0 > 0:
                     nc.vector.tensor_copy(wins[b][:, e0 * C : e1 * C], y[:])
                 else:
                     nc.scalar.activation(wins[b][:, e0 * C : e1 * C], y[:], ACT.Copy)
@@ -192,7 +202,7 @@ def tile_moe_cpy_mlp_relu2_kernel(
                             stop=(r == 1 and q == T // P - 1),
                             is_transpose=True,
                         )
-                total_sb = ring.tile([P, T // P, P], F32, name="pos")
+                total_sb = ring.tile([P, T // P, P], F32, name="total_sb")
                 nc.scalar.activation(total_sb[:], total[:], ACT.Copy)
                 back = psum.tile([P, T // P, P], F32, name="turned")
                 for q in range(T // P):
@@ -202,14 +212,12 @@ def tile_moe_cpy_mlp_relu2_kernel(
                 nc.vector.tensor_tensor(res[:], first[:], second[:], ALU.add)
             nc.sync.dma_start(out[b * P : (b + 1) * P, t0:t1], res[:])
 
-        second_layer(0)
-        second_layer(1)
+        for b in range(BLOCKS):
+            second_layer(b)
 
         pieces = [(b, 0, T) for b in range(BLOCKS - 1)] + [(BLOCKS - 1, 0, T // 2), (BLOCKS - 1, T // 2, T)]
         waiting = None
         for b, t0, t1 in pieces:
-            if t0 == 0 and b + 2 < BLOCKS:
-                second_layer(b + 2)
             idx = slice(t0 // 16, t1 // 16)
             first = prods.tile([P, t1 - t0], F32, name="first")
             nc.vector.tensor_tensor(first[:], wins[b][:].indirect(pos1_sb[:, idx]), gates[:, 0, t0:t1], ALU.mult)

@@ -22,10 +22,15 @@ PASSES = K // (P * PACK)
 SLOTS = E * C
 BLOCKS = K // P
 WINDOW = SLOTS + T + PAD
-TENSOR_ADDS = 6
-GATHER_EXPERTS = [(0, 1), (1, 3), (3, 5), (5, 6)]
-W1_LOADS = [(0, 1), (1, 3), (3, 6)]
-VECTOR_RELU_FROM = 3
+TENSOR_ADDS = 7
+GATHER_EXPERTS = [(0, 1), (1, 2), (2, 4), (4, 5), (5, 6)]
+W1_LOADS = [(0, 1), (1, 2), (2, 4), (4, 6)]
+FIRST_EXPERTS = 2
+W2_LOADS = [(0, 2), (2, 5), (5, 8)]
+QUANTIZE_EXPERTS = [(0, 4), (4, 5), (5, 6)]
+VECTOR_RELU_FROM = 4
+EARLY_BLOCKS = 2
+BLOCKS_BEFORE_SUMS = 5
 
 
 def tile_moe_cpy_mlp_relu2_kernel(
@@ -36,35 +41,50 @@ def tile_moe_cpy_mlp_relu2_kernel(
         keep = ctx.enter_context(tc.tile_pool(name="keep", bufs=1))
         ring = ctx.enter_context(tc.tile_pool(name="ring", bufs=3))
         prods = ctx.enter_context(tc.tile_pool(name="prods", bufs=8))
-        psum = ctx.enter_context(tc.psum_pool(name="psum", bufs=2))
+        psum = ctx.enter_context(tc.psum_pool(name="psum", bufs=3))
 
         offs_sb = keep.tile([P, SLOTS // 16], U16, name="offs_sb")
         pos1_sb = keep.tile([P, T // 16], U16, name="pos1_sb")
         pos2_sb = keep.tile([P, T // 16], U16, name="pos2_sb")
         xw = keep.tile([P, PASSES, T], I32, name="xw", align_bytes=64)
         xs = keep.tile([P, PASSES, T // 4], I32, name="xs", align_bytes=64)
-        w1s = keep.tile([P, E * PASSES, H // 4], I32, name="w1s", align_bytes=64)
+        plane_a = keep.tile([P, FIRST_EXPERTS * K // 4], I32, name="plane_a", align_bytes=64)
+        plane_b = keep.tile([P, E * (BLOCKS - EARLY_BLOCKS) * P // 4], I32, name="plane_b", align_bytes=64)
         ident = keep.tile([P, P], F32, name="ident")
         zeros = keep.tile([P, PAD], F32, name="zeros")
-        w2s = keep.tile([P, E, K // 4], I32, name="w2s", align_bytes=64)
         hb = keep.tile([P, SLOTS, PACK], BF16, name="hb", align_bytes=64)
         hq = keep.tile([P, SLOTS], U32, name="hq", align_bytes=64)
         hs = keep.tile([P, SLOTS], U8, name="hs", align_bytes=64)
 
         def load_scales(plane, rows):
             for r in range(4):
-                nc.sync.dma_start(plane[r:P:32, :, :], rows[r].bitcast(I32))
+                nc.sync.dma_start(plane[r:P:32], rows[r].bitcast(I32))
 
-        nc.gpsimd.memset(xs[:], 0)
+        w1 = []
+
+        def load_w1(pool, n):
+            e0, e1 = W1_LOADS[n]
+            tile = pool.tile([P, (e1 - e0) * PASSES, 2 * H], U8, name=f"w1_{n}", tag=f"slot{n}", align_bytes=64)
+            nc.sync.dma_start(tile[:].bitcast(I32), w1_words[e0:e1].rearrange("e s p c -> p (e s) c").bitcast(I32))
+            w1.extend(tile[:, (e - e0) * PASSES : (e - e0 + 1) * PASSES, :] for e in range(e0, e1))
+
+        w1s_a = plane_a[:].rearrange("p (g i) -> p g i", i=H // 4)
+        w1s_b = plane_b[:, : (E - FIRST_EXPERTS) * K // 4].rearrange("p (g i) -> p g i", i=H // 4)
+        w1_rows = w1_scales.rearrange("e s (q r) i -> r q (e s) i", r=4)
+        head = FIRST_EXPERTS * PASSES
+        nc.vector.memset(xs[:], 0)
+        nc.gpsimd.memset(plane_a[:], 0)
         nc.gpsimd.memset(zeros[:], 0.0)
-        nc.vector.memset(w1s[:], 0)
+        nc.vector.memset(plane_b[:], 0)
         nc.sync.dma_start(offs_sb[:], offs)
-        for s in range(PASSES):
-            nc.sync.dma_start(xw[:, s, :], x_words[s].rearrange("p t d -> p (t d)").bitcast(I32))
-        load_scales(xs, x_scales.rearrange("s (q r) t -> r q s t", r=4))
-        load_scales(w1s, w1_scales.rearrange("e s (q r) i -> r q (e s) i", r=4))
         nc.sync.dma_start(pos1_sb[:], pos1)
         nc.sync.dma_start(pos2_sb[:], pos2)
+        load_scales(xs, x_scales.rearrange("s (q r) t -> r q s t", r=4))
+        nc.sync.dma_start(xw[:], x_words.rearrange("s p t d -> p s (t d)").bitcast(I32))
+        load_w1(keep, 0)
+        load_scales(w1s_a, [w1_rows[r][:, :head, :] for r in range(4)])
+        load_w1(keep, 1)
+        load_scales(w1s_b, [w1_rows[r][:, head:, :] for r in range(4)])
 
         with tc.tile_pool(name="setup", bufs=1) as setup:
             blank = setup.tile([P, P], F32, name="blank")
@@ -84,17 +104,18 @@ def tile_moe_cpy_mlp_relu2_kernel(
         def load_xr(win, b):
             nc.sync.dma_start(win[:, SLOTS : SLOTS + T], xr[b * P : (b + 1) * P, :])
 
-        def load_w2(tile, hf):
-            src = w2_words.rearrange("e o p c -> p (e o) c")[:, :, hf * K : (hf + 1) * K]
-            nc.sync.dma_start(tile[:].bitcast(I32), src.bitcast(I32))
+        w2 = []
 
-        w1 = []
-        for n, (e0, e1) in enumerate(W1_LOADS):
-            tile = big.tile([P, (e1 - e0) * PASSES, 2 * H], U8, name=f"w1_{n}", tag=f"slot{n}", align_bytes=64)
-            nc.sync.dma_start(tile[:].bitcast(I32), w1_words[e0:e1].rearrange("e s p c -> p (e s) c").bitcast(I32))
-            w1 += [tile[:, (e - e0) * PASSES : (e - e0 + 1) * PASSES, :] for e in range(e0, e1)]
-        nc.vector.memset(w2s[:], 0)
-        load_scales(w2s, w2_scales.rearrange("e o (q r) n -> r q (e o) n", r=4))
+        def load_w2(pool, n, tag):
+            b0, b1 = W2_LOADS[n]
+            tile = pool.tile([P, E, (b1 - b0) * 2 * P], U8, name=f"w2_{n}", tag=tag, align_bytes=64)
+            src = w2_words.rearrange("e o p c -> p (e o) c")[:, :, b0 * 2 * P : b1 * 2 * P]
+            nc.sync.dma_start(tile[:].bitcast(I32), src.bitcast(I32))
+            w2.extend(tile[:, :, (b - b0) * 2 * P : (b - b0 + 1) * 2 * P] for b in range(b0, b1))
+
+        for n in range(2, len(W1_LOADS)):
+            load_w1(big, n)
+        load_w2(big, 0, "w2_first")
         wins = [big.tile([P, WINDOW], F32, name="win0")]
         load_xr(wins[0], 0)
         nc.scalar.activation(wins[0][:, SLOTS + T :], zeros[:], ACT.Copy)
@@ -104,80 +125,86 @@ def tile_moe_cpy_mlp_relu2_kernel(
             for e0, e1 in GATHER_EXPERTS:
                 width = (e1 - e0) * C
                 idx = offs_sb[:, e0 * C // 16 : e1 * C // 16]
-                xg = [gathered.tile([P, width], U32, name=f"xg{s}", align_bytes=64) for s in range(PASSES)]
-                sg = [gathered.tile([P, width], U8, name=f"sg{s}", align_bytes=64, bufs=3) for s in range(PASSES)]
-                for s in range(PASSES):
-                    nc.vector.tensor_copy(xg[s][:], xw[:, s, :].bitcast(U32).indirect(idx))
+                xg = [gathered.tile([P, width], U32, name=f"xg{s}", align_bytes=64, bufs=3) for s in range(PASSES)]
+                sg = [gathered.tile([P, width], U8, name=f"sg{s}", align_bytes=64, bufs=2) for s in range(PASSES)]
                 for s in range(PASSES):
                     nc.vector.tensor_copy(sg[s][:], xs[:, s, :].bitcast(U8).indirect(idx))
+                for s in range(PASSES):
+                    nc.vector.tensor_copy(xg[s][:], xw[:, s, :].bitcast(U32).indirect(idx))
                 tokens += [(xg, sg, slice((e - e0) * C, (e - e0 + 1) * C)) for e in range(e0, e1)]
+
+            def turn_and_square(e, pos):
+                cols = slice(e * C, (e + 1) * C)
+                turned = psum.tile([P, PACK, C], F32, name="turned", tag="turns")
+                for d in range(PACK):
+                    nc.tensor.transpose(turned[:, d, :], pos[:, d, :], ident[:])
+                nc.scalar.activation(hb[:, cols, :], turned[:].rearrange("p d s -> p s d"), ACT.Square)
+                for e0, e1 in QUANTIZE_EXPERTS:
+                    if e1 == e + 1:
+                        done = slice(e0 * C, e1 * C)
+                        nc.vector.quantize_mx(
+                            out=hq[:, done].bitcast(FP8X4),
+                            scales=hs[:, done],
+                            in_=hb[:, done, :].rearrange("p u j -> p (u j)"),
+                        )
 
             positive = []
             for e in range(E):
                 xg, sg, own = tokens[e]
-                pre = psum.tile([P, H], F32, name="pre", bufs=3)
+                pre = psum.tile([P, H], F32, name="pre", tag="sums")
                 for s in range(PASSES):
                     nc.tensor.matmul_mx(
                         out=pre[:],
                         lhsT=xg[s][:, own].bitcast(FP8X4),
                         lhsT_scale=sg[s][:, own],
                         rhs=w1[e][:, s, :].bitcast(FP4X4),
-                        rhs_scale=w1s[:, e * PASSES + s, :].bitcast(U8),
+                        rhs_scale=(w1s_a[:, e * PASSES + s, :] if e < FIRST_EXPERTS else w1s_b[:, e * PASSES + s - head, :]).bitcast(U8),
                         start=(s == 0),
                         stop=(s == PASSES - 1),
                     )
-                pos = ring.tile([P, 2, P, 2], F32, name="pos", bufs=E)
-                positive.append(pos)
-                by_pair = pre[:].rearrange("p (m u c) -> p u m c", u=2, c=2)
-                if e >= VECTOR_RELU_FROM:
-                    nc.vector.tensor_scalar_max(pos[:], by_pair, 0.0)
+                pos = ring.tile([P, PACK, P], F32, name="pos", bufs=E)
+                by_place = pos[:].rearrange("p d m -> p m d")
+                sums = pre[:].rearrange("p (m d) -> p m d", d=PACK)
+                if e < VECTOR_RELU_FROM:
+                    nc.scalar.activation(by_place, sums, ACT.Relu)
                 else:
-                    nc.scalar.activation(pos[:], by_pair, ACT.Relu)
+                    nc.vector.tensor_scalar_max(by_place, sums, 0.0)
+                positive.append(pos)
+            for e, pos in enumerate(positive):
+                turn_and_square(e, pos)
 
-        for e, pos in enumerate(positive):
-            cols = slice(e * C, (e + 1) * C)
-            h = ring.tile([P, 2, 2 * P], BF16, name="h")
-            nc.scalar.activation(h[:], pos[:].rearrange("p u m c -> p u (m c)"), ACT.Square)
-            turned = psum.tile([P, 2, C], F32, name="turned")
-            for u in range(2):
-                nc.tensor.transpose(turned[:, u, :], h[:, u, :].bitcast(F32), ident[:])
-            pairs = hb[:, cols, :].bitcast(F32)
-            if e >= VECTOR_RELU_FROM:
-                nc.vector.tensor_copy(pairs, turned[:].rearrange("p u s -> p s u"))
-            else:
-                nc.scalar.copy(pairs, turned[:].rearrange("p u s -> p s u"))
-
-        w2 = [big.tile([P, E, K], U8, name="w2_0", tag="slot0", align_bytes=64)]
-        load_w2(w2[0], 0)
-        gates = big.tile([P, 2, T], F32, name="gates", tag="slot1", align_bytes=64)
-        nc.sync.dma_start(gates[:], gate.rearrange("r p t -> p r t"))
+        w2_rows = w2_scales.rearrange("e o (q r) n -> r q (e o) n", r=4)
+        cut = EARLY_BLOCKS * P
+        early = plane_a[:, : E * cut // 4].rearrange("p (e n) -> p e n", e=E)
+        rest = plane_b[:].rearrange("p (e n) -> p e n", e=E)
+        load_scales(early, [w2_rows[r][:, :, :cut] for r in range(4)])
+        gates = keep.tile([P, 2, T], F32, name="gates", tag="slot1", align_bytes=64)
+        for r in range(2):
+            nc.sync.dma_start(gates[:, r, :], gate[r])
+        load_w2(big, 1, "slot2")
         late = ctx.enter_context(tc.tile_pool(name="late", bufs=1, side="right"))
+        load_scales(rest, [w2_rows[r][:, :, cut:] for r in range(4)])
         for b in range(1, BLOCKS):
             wins.append(late.tile([P, WINDOW], F32, name=f"win{b}"))
             load_xr(wins[b], b)
             nc.gpsimd.memset(wins[b][:, SLOTS + T :], 0.0)
             if b == 1:
-                w2.append(late.tile([P, E, K], U8, name="w2_1", align_bytes=64))
-                load_w2(w2[1], 1)
+                load_w2(late, 2, "w2_last")
 
-        for e0, e1 in ((0, 4), (4, 5), (5, 6)):
-            done = slice(e0 * C, e1 * C)
-            nc.vector.quantize_mx(
-                out=hq[:, done].bitcast(FP8X4),
-                scales=hs[:, done],
-                in_=hb[:, done, :].rearrange("p u j -> p (u j)"),
-            )
+        def w2_scale(e, b):
+            if b < EARLY_BLOCKS:
+                return early[:, e, b * P // 4 : (b + 1) * P // 4].bitcast(U8)
+            return rest[:, e, (b - EARLY_BLOCKS) * P // 4 : (b - EARLY_BLOCKS + 1) * P // 4].bitcast(U8)
 
         def second_layer(b):
-            hf, c0 = divmod(b * P, K // 2)
-            for name, e0, e1, depth in (("ya", 0, 4, 2), ("yb", 4, E, 1)):
-                y = psum.tile([P, (e1 - e0) * C], F32, name=name, bufs=depth)
+            for tag, e0, e1, depth in (("sums", 0, 4, 3), ("small", 4, E, 2)):
+                y = psum.tile([P, (e1 - e0) * C], F32, name="y", tag=tag, bufs=depth)
                 for e in range(e0, e1):
                     cols = slice(e * C, (e + 1) * C)
                     nc.tensor.matmul_mx(
                         out=y[:, (e - e0) * C : (e - e0 + 1) * C],
-                        lhsT=w2[hf][:, e, 2 * c0 : 2 * (c0 + P)].bitcast(FP4X4),
-                        lhsT_scale=w2s[:, e, b * P // 4 : (b + 1) * P // 4].bitcast(U8),
+                        lhsT=w2[b][:, e, :].bitcast(FP4X4),
+                        lhsT_scale=w2_scale(e, b),
                         rhs=hq[:, cols].bitcast(FP8X4),
                         rhs_scale=hs[:, cols],
                         start=True,
@@ -191,7 +218,7 @@ def tile_moe_cpy_mlp_relu2_kernel(
         def add_and_store(b, t0, t1, first, second):
             res = ring.tile([P, t1 - t0], F32, name="res", bufs=BLOCKS + 1)
             if b < TENSOR_ADDS:
-                total = psum.tile([P, T // P, P], F32, name="pre", bufs=3)
+                total = psum.tile([P, T // P, P], F32, name="total", tag="sums")
                 for r, term in enumerate((first, second)):
                     for q in range(T // P):
                         nc.tensor.matmul(
@@ -204,15 +231,18 @@ def tile_moe_cpy_mlp_relu2_kernel(
                         )
                 total_sb = ring.tile([P, T // P, P], F32, name="total_sb")
                 nc.scalar.activation(total_sb[:], total[:], ACT.Copy)
-                back = psum.tile([P, T // P, P], F32, name="turned")
+                back = psum.tile([P, T // P, P], F32, name="back", tag="turns")
                 for q in range(T // P):
                     nc.tensor.transpose(back[:, q, :], total_sb[:, q, :], ident[:])
                 nc.scalar.activation(res[:], back[:].rearrange("p q t -> p (q t)"), ACT.Copy)
             else:
                 nc.vector.tensor_tensor(res[:], first[:], second[:], ALU.add)
             nc.sync.dma_start(out[b * P : (b + 1) * P, t0:t1], res[:])
+            if b == 0:
+                for later in range(BLOCKS_BEFORE_SUMS, BLOCKS):
+                    second_layer(later)
 
-        for b in range(BLOCKS):
+        for b in range(BLOCKS_BEFORE_SUMS):
             second_layer(b)
 
         pieces = [(b, 0, T) for b in range(BLOCKS - 1)] + [(BLOCKS - 1, 0, T // 2), (BLOCKS - 1, T // 2, T)]

@@ -22,7 +22,7 @@ PASSES = K // (P * PACK)
 SLOTS = E * C
 BLOCKS = K // P
 WINDOW = SLOTS + T + PAD
-TENSOR_ADDS = 7
+TENSOR_ADDS = 6
 GATHER_EXPERTS = [(0, 1), (1, 2), (2, 4), (4, 5), (5, 6)]
 W1_LOADS = [(0, 1), (1, 2), (2, 4), (4, 6)]
 FIRST_EXPERTS = 2

@@ -23,14 +23,19 @@ SLOTS = E * C
 BLOCKS = K // P
 WINDOW = SLOTS + T + PAD
 TENSOR_ADDS = 6
-GATHER_EXPERTS = [(0, 1), (1, 2), (2, 4), (4, 5), (5, 6)]
+WORD_PIECES = [(0, 1), (1, 2), (2, 4), (4, 5), (5, 6)]
+BYTE_PIECES = [(0, 1), (1, 2), (2, 4), (4, 6)]
 W1_LOADS = [(0, 1), (1, 2), (2, 4), (4, 6)]
 FIRST_EXPERTS = 2
 W2_LOADS = [(0, 2), (2, 5), (5, 8)]
-QUANTIZE_EXPERTS = [(0, 4), (4, 5), (5, 6)]
+QUANTIZE_EXPERTS = [(0, 2), (2, 4), (4, 5), (5, 6)]
+WORD_TURNED = 4
 VECTOR_RELU_FROM = 4
 EARLY_BLOCKS = 2
+WARM_PASSES = 6
+RUN = 2 * T // P
 BLOCKS_BEFORE_SUMS = 5
+BLOCKS_ON_PAIR = (3, 4, 6, 7)
 
 
 def tile_moe_cpy_mlp_relu2_kernel(
@@ -46,7 +51,7 @@ def tile_moe_cpy_mlp_relu2_kernel(
         offs_sb = keep.tile([P, SLOTS // 16], U16, name="offs_sb")
         pos1_sb = keep.tile([P, T // 16], U16, name="pos1_sb")
         pos2_sb = keep.tile([P, T // 16], U16, name="pos2_sb")
-        xw = keep.tile([P, PASSES, T], I32, name="xw", align_bytes=64)
+        xw = [keep.tile([P, T], I32, name=f"xw{s}", align_bytes=64) for s in range(PASSES)]
         xs = keep.tile([P, PASSES, T // 4], I32, name="xs", align_bytes=64)
         plane_a = keep.tile([P, FIRST_EXPERTS * K // 4], I32, name="plane_a", align_bytes=64)
         plane_b = keep.tile([P, E * (BLOCKS - EARLY_BLOCKS) * P // 4], I32, name="plane_b", align_bytes=64)
@@ -77,14 +82,17 @@ def tile_moe_cpy_mlp_relu2_kernel(
         nc.gpsimd.memset(zeros[:], 0.0)
         nc.vector.memset(plane_b[:], 0)
         nc.sync.dma_start(offs_sb[:], offs)
-        nc.sync.dma_start(pos1_sb[:], pos1)
-        nc.sync.dma_start(pos2_sb[:], pos2)
+        nc.sync.dma_start(xw[0][:], x_words[0].rearrange("p t d -> p (t d)").bitcast(I32))
+        gate_row = keep.tile([P, RUN], F32, name="gate_row")
+        nc.sync.dma_start(gate_row[:], gate[:, 0, :].rearrange("r (n j) -> r n j", j=RUN))
         load_scales(xs, x_scales.rearrange("s (q r) t -> r q s t", r=4))
-        nc.sync.dma_start(xw[:], x_words.rearrange("s p t d -> p s (t d)").bitcast(I32))
+        nc.sync.dma_start(xw[1][:], x_words[1].rearrange("p t d -> p (t d)").bitcast(I32))
         load_w1(keep, 0)
         load_scales(w1s_a, [w1_rows[r][:, :head, :] for r in range(4)])
         load_w1(keep, 1)
         load_scales(w1s_b, [w1_rows[r][:, head:, :] for r in range(4)])
+        nc.sync.dma_start(pos1_sb[:], pos1)
+        nc.sync.dma_start(pos2_sb[:], pos2)
 
         with tc.tile_pool(name="setup", bufs=1) as setup:
             blank = setup.tile([P, P], F32, name="blank")
@@ -101,6 +109,31 @@ def tile_moe_cpy_mlp_relu2_kernel(
 
         big = ctx.enter_context(tc.tile_pool(name="big", bufs=1))
 
+        first_w2 = keep.tile([P, E, EARLY_BLOCKS * 2 * P], U8, name="first_w2", align_bytes=64)
+        warm_words = first_w2[:, :2, :].rearrange("p e c -> p (e c)")
+        nc.vector.memset(warm_words.bitcast(I32), 0)
+        nc.vector.memset(hq[:, :P].bitcast(I32), 0)
+        nc.vector.memset(hs[:, : H + P].bitcast(I32), 0)
+        warm = psum.tile([P, H], F32, name="warm", tag="single", bufs=1)
+        for n in range(WARM_PASSES):
+            nc.tensor.matmul_mx(
+                out=warm[:],
+                lhsT=hq[:, :P].bitcast(FP8X4),
+                lhsT_scale=hs[:, H : H + P],
+                rhs=warm_words.bitcast(FP4X4),
+                rhs_scale=hs[:, :H],
+                start=True,
+                stop=True,
+            )
+
+        gates = keep.tile([P, 2, T], F32, name="gates", align_bytes=64)
+        by_run = gates[:].rearrange("p r (n j) -> p (r n) j", j=RUN)
+        for j0 in range(0, RUN, PACK):
+            spread = psum.tile([P, PACK, P], F32, name="spread", tag="pair" if j0 else "single", bufs=2 if j0 else 1)
+            for j in range(PACK):
+                nc.tensor.transpose(spread[:, j, :], gate_row[:, j0 + j : j0 + j + 1].to_broadcast([P, P]), ident[:])
+            nc.scalar.activation(by_run[:, :, j0 : j0 + PACK], spread[:].rearrange("p j n -> p n j"), ACT.Copy)
+
         def load_xr(win, b):
             nc.sync.dma_start(win[:, SLOTS : SLOTS + T], xr[b * P : (b + 1) * P, :])
 
@@ -108,37 +141,48 @@ def tile_moe_cpy_mlp_relu2_kernel(
 
         def load_w2(pool, n, tag):
             b0, b1 = W2_LOADS[n]
-            tile = pool.tile([P, E, (b1 - b0) * 2 * P], U8, name=f"w2_{n}", tag=tag, align_bytes=64)
+            tile = pool.tile([P, E, (b1 - b0) * 2 * P], U8, name=f"w2_{n}", tag=tag, align_bytes=64) if pool else tag
             src = w2_words.rearrange("e o p c -> p (e o) c")[:, :, b0 * 2 * P : b1 * 2 * P]
             nc.sync.dma_start(tile[:].bitcast(I32), src.bitcast(I32))
             w2.extend(tile[:, :, (b - b0) * 2 * P : (b - b0 + 1) * 2 * P] for b in range(b0, b1))
 
         for n in range(2, len(W1_LOADS)):
             load_w1(big, n)
-        load_w2(big, 0, "w2_first")
+        load_w2(None, 0, first_w2)
         wins = [big.tile([P, WINDOW], F32, name="win0")]
         load_xr(wins[0], 0)
         nc.scalar.activation(wins[0][:, SLOTS + T :], zeros[:], ACT.Copy)
 
         with tc.tile_pool(name="gathered", bufs=2, side="right") as gathered:
-            tokens = []
-            for e0, e1 in GATHER_EXPERTS:
-                width = (e1 - e0) * C
+            words, scale_bytes = [], []
+
+            def gather(pieces, n, name, dtype, depth, window, found):
+                e0, e1 = pieces[n]
                 idx = offs_sb[:, e0 * C // 16 : e1 * C // 16]
-                xg = [gathered.tile([P, width], U32, name=f"xg{s}", align_bytes=64, bufs=3) for s in range(PASSES)]
-                sg = [gathered.tile([P, width], U8, name=f"sg{s}", align_bytes=64, bufs=2) for s in range(PASSES)]
+                tiles = [gathered.tile([P, (e1 - e0) * C], dtype, name=f"{name}{s}", align_bytes=64, bufs=depth) for s in range(PASSES)]
                 for s in range(PASSES):
-                    nc.vector.tensor_copy(sg[s][:], xs[:, s, :].bitcast(U8).indirect(idx))
-                for s in range(PASSES):
-                    nc.vector.tensor_copy(xg[s][:], xw[:, s, :].bitcast(U32).indirect(idx))
-                tokens += [(xg, sg, slice((e - e0) * C, (e - e0 + 1) * C)) for e in range(e0, e1)]
+                    nc.vector.tensor_copy(tiles[s][:], window(s).bitcast(dtype).indirect(idx))
+                found.extend([t[:, (e - e0) * C : (e - e0 + 1) * C] for t in tiles] for e in range(e0, e1))
+
+            for n in range(len(WORD_PIECES)):
+                if n < len(BYTE_PIECES):
+                    gather(BYTE_PIECES, n, "sg", U8, 2, lambda s: xs[:, s, :], scale_bytes)
+                gather(WORD_PIECES, n, "xg", U32, 3, lambda s: xw[s][:], words)
 
             def turn_and_square(e, pos):
                 cols = slice(e * C, (e + 1) * C)
-                turned = psum.tile([P, PACK, C], F32, name="turned", tag="turns")
-                for d in range(PACK):
-                    nc.tensor.transpose(turned[:, d, :], pos[:, d, :], ident[:])
-                nc.scalar.activation(hb[:, cols, :], turned[:].rearrange("p d s -> p s d"), ACT.Square)
+                turned = psum.tile([P, PACK, C], F32, name="turned", tag="pair" if e % 3 else "single", bufs=2 if e % 3 else 1)
+                if e == WORD_TURNED:
+                    h = ring.tile([P, 2, 2 * P], BF16, name="h", bufs=1)
+                    flat = pos[:].rearrange("p (u a) m -> p u (a m)", u=2)
+                    nc.vector.tensor_tensor(h[:], flat, flat, ALU.mult)
+                    for u in range(2):
+                        nc.tensor.transpose(turned[:, u, :], h[:, u, :].bitcast(F32), ident[:])
+                    nc.vector.tensor_copy(hb[:, cols, :].bitcast(F32), turned[:, :2, :].rearrange("p u s -> p s u"))
+                else:
+                    for d in range(PACK):
+                        nc.tensor.transpose(turned[:, d, :], pos[:, d, :], ident[:])
+                    nc.scalar.activation(hb[:, cols, :], turned[:].rearrange("p d s -> p s d"), ACT.Square)
                 for e0, e1 in QUANTIZE_EXPERTS:
                     if e1 == e + 1:
                         done = slice(e0 * C, e1 * C)
@@ -149,14 +193,14 @@ def tile_moe_cpy_mlp_relu2_kernel(
                         )
 
             positive = []
+            turns_after = {1: (0, 1), 5: (2, 3, 5, 4)}
             for e in range(E):
-                xg, sg, own = tokens[e]
                 pre = psum.tile([P, H], F32, name="pre", tag="sums")
                 for s in range(PASSES):
                     nc.tensor.matmul_mx(
                         out=pre[:],
-                        lhsT=xg[s][:, own].bitcast(FP8X4),
-                        lhsT_scale=sg[s][:, own],
+                        lhsT=words[e][s].bitcast(FP8X4),
+                        lhsT_scale=scale_bytes[e][s],
                         rhs=w1[e][:, s, :].bitcast(FP4X4),
                         rhs_scale=(w1s_a[:, e * PASSES + s, :] if e < FIRST_EXPERTS else w1s_b[:, e * PASSES + s - head, :]).bitcast(U8),
                         start=(s == 0),
@@ -165,22 +209,22 @@ def tile_moe_cpy_mlp_relu2_kernel(
                 pos = ring.tile([P, PACK, P], F32, name="pos", bufs=E)
                 by_place = pos[:].rearrange("p d m -> p m d")
                 sums = pre[:].rearrange("p (m d) -> p m d", d=PACK)
+                if e == WORD_TURNED:
+                    by_place = pos[:].rearrange("p d m -> p (d m)").rearrange("p (u m c) -> p u m c", u=2, c=2)
+                    sums = pre[:].rearrange("p (m u c) -> p u m c", u=2, c=2)
                 if e < VECTOR_RELU_FROM:
                     nc.scalar.activation(by_place, sums, ACT.Relu)
                 else:
                     nc.vector.tensor_scalar_max(by_place, sums, 0.0)
                 positive.append(pos)
-            for e, pos in enumerate(positive):
-                turn_and_square(e, pos)
+                for done in turns_after.get(e, ()):
+                    turn_and_square(done, positive[done])
 
         w2_rows = w2_scales.rearrange("e o (q r) n -> r q (e o) n", r=4)
         cut = EARLY_BLOCKS * P
         early = plane_a[:, : E * cut // 4].rearrange("p (e n) -> p e n", e=E)
         rest = plane_b[:].rearrange("p (e n) -> p e n", e=E)
         load_scales(early, [w2_rows[r][:, :, :cut] for r in range(4)])
-        gates = keep.tile([P, 2, T], F32, name="gates", tag="slot1", align_bytes=64)
-        for r in range(2):
-            nc.sync.dma_start(gates[:, r, :], gate[r])
         load_w2(big, 1, "slot2")
         late = ctx.enter_context(tc.tile_pool(name="late", bufs=1, side="right"))
         load_scales(rest, [w2_rows[r][:, :, cut:] for r in range(4)])
@@ -197,7 +241,9 @@ def tile_moe_cpy_mlp_relu2_kernel(
             return rest[:, e, (b - EARLY_BLOCKS) * P // 4 : (b - EARLY_BLOCKS + 1) * P // 4].bitcast(U8)
 
         def second_layer(b):
-            for tag, e0, e1, depth in (("sums", 0, 4, 3), ("small", 4, E, 2)):
+            wide = ("sums", 0, 4, 3) if b not in BLOCKS_ON_PAIR else ("pair", 0, 4, 2)
+            narrow = [("small", 4, 5, 2), ("small", 5, E, 2)] if b == 0 else [("small", 4, E, 2)]
+            for tag, e0, e1, depth in [wide] + narrow:
                 y = psum.tile([P, (e1 - e0) * C], F32, name="y", tag=tag, bufs=depth)
                 for e in range(e0, e1):
                     cols = slice(e * C, (e + 1) * C)
@@ -218,7 +264,7 @@ def tile_moe_cpy_mlp_relu2_kernel(
         def add_and_store(b, t0, t1, first, second):
             res = ring.tile([P, t1 - t0], F32, name="res", bufs=BLOCKS + 1)
             if b < TENSOR_ADDS:
-                total = psum.tile([P, T // P, P], F32, name="total", tag="sums")
+                total = psum.tile([P, T // P, P], F32, name="total", tag="pair", bufs=2)
                 for r, term in enumerate((first, second)):
                     for q in range(T // P):
                         nc.tensor.matmul(
@@ -231,7 +277,7 @@ def tile_moe_cpy_mlp_relu2_kernel(
                         )
                 total_sb = ring.tile([P, T // P, P], F32, name="total_sb")
                 nc.scalar.activation(total_sb[:], total[:], ACT.Copy)
-                back = psum.tile([P, T // P, P], F32, name="back", tag="turns")
+                back = psum.tile([P, T // P, P], F32, name="back", tag="small", bufs=2)
                 for q in range(T // P):
                     nc.tensor.transpose(back[:, q, :], total_sb[:, q, :], ident[:])
                 nc.scalar.activation(res[:], back[:].rearrange("p q t -> p (q t)"), ACT.Copy)

@@ -78,6 +78,11 @@ def tile_moe_cpy_mlp_relu2_kernel(
         w1_rows = w1_scales.rearrange("e s (q r) i -> r q (e s) i", r=4)
         head = FIRST_EXPERTS * PASSES
         nc.vector.memset(xs[:], 0)
+        first_w2 = keep.tile([P, E, EARLY_BLOCKS * 2 * P], U8, name="first_w2", align_bytes=64)
+        warm_words = first_w2[:, :2, :].rearrange("p e c -> p (e c)")
+        nc.vector.memset(warm_words.bitcast(I32), 0)
+        nc.vector.memset(hq[:, :P].bitcast(I32), 0)
+        nc.vector.memset(hs[:, :H].bitcast(I32), 0)
         nc.gpsimd.memset(plane_a[:], 0)
         nc.gpsimd.memset(zeros[:], 0.0)
         nc.vector.memset(plane_b[:], 0)
@@ -109,17 +114,12 @@ def tile_moe_cpy_mlp_relu2_kernel(
 
         big = ctx.enter_context(tc.tile_pool(name="big", bufs=1))
 
-        first_w2 = keep.tile([P, E, EARLY_BLOCKS * 2 * P], U8, name="first_w2", align_bytes=64)
-        warm_words = first_w2[:, :2, :].rearrange("p e c -> p (e c)")
-        nc.vector.memset(warm_words.bitcast(I32), 0)
-        nc.vector.memset(hq[:, :P].bitcast(I32), 0)
-        nc.vector.memset(hs[:, : H + P].bitcast(I32), 0)
         warm = psum.tile([P, H], F32, name="warm", tag="single", bufs=1)
         for n in range(WARM_PASSES):
             nc.tensor.matmul_mx(
                 out=warm[:],
                 lhsT=hq[:, :P].bitcast(FP8X4),
-                lhsT_scale=hs[:, H : H + P],
+                lhsT_scale=hs[:, :P],
                 rhs=warm_words.bitcast(FP4X4),
                 rhs_scale=hs[:, :H],
                 start=True,
@@ -262,28 +262,30 @@ def tile_moe_cpy_mlp_relu2_kernel(
                     nc.scalar.activation(wins[b][:, e0 * C : e1 * C], y[:], ACT.Copy)
 
         def add_and_store(b, t0, t1, first, second):
-            res = ring.tile([P, t1 - t0], F32, name="res", bufs=BLOCKS + 1)
-            if b < TENSOR_ADDS:
-                total = psum.tile([P, T // P, P], F32, name="total", tag="pair", bufs=2)
+            res = ring.tile([P, t1 - t0], F32, name="res", bufs=BLOCKS + 2)
+            if b < TENSOR_ADDS or (b == TENSOR_ADDS and t0 == 0):
+                parts = (t1 - t0) // P
+                total = psum.tile([P, parts, P], F32, name="total", tag="pair", bufs=2)
                 for r, term in enumerate((first, second)):
-                    for q in range(T // P):
+                    for q in range(parts):
                         nc.tensor.matmul(
                             total[:, q, :],
                             term[:, q * P : (q + 1) * P],
                             ident[:],
                             start=(r == 0 and q == 0),
-                            stop=(r == 1 and q == T // P - 1),
+                            stop=(r == 1 and q == parts - 1),
                             is_transpose=True,
                         )
-                total_sb = ring.tile([P, T // P, P], F32, name="total_sb")
+                total_sb = ring.tile([P, parts, P], F32, name="total_sb")
                 nc.scalar.activation(total_sb[:], total[:], ACT.Copy)
-                back = psum.tile([P, T // P, P], F32, name="back", tag="small", bufs=2)
-                for q in range(T // P):
+                back = psum.tile([P, parts, P], F32, name="back", tag="small", bufs=2)
+                for q in range(parts):
                     nc.tensor.transpose(back[:, q, :], total_sb[:, q, :], ident[:])
                 nc.scalar.activation(res[:], back[:].rearrange("p q t -> p (q t)"), ACT.Copy)
+                nc.scalar.dma_start(out[b * P : (b + 1) * P, t0:t1], res[:])
             else:
                 nc.vector.tensor_tensor(res[:], first[:], second[:], ALU.add)
-            nc.sync.dma_start(out[b * P : (b + 1) * P, t0:t1], res[:])
+                nc.sync.dma_start(out[b * P : (b + 1) * P, t0:t1], res[:])
             if b == 0:
                 for later in range(BLOCKS_BEFORE_SUMS, BLOCKS):
                     second_layer(later)
@@ -291,7 +293,8 @@ def tile_moe_cpy_mlp_relu2_kernel(
         for b in range(BLOCKS_BEFORE_SUMS):
             second_layer(b)
 
-        pieces = [(b, 0, T) for b in range(BLOCKS - 1)] + [(BLOCKS - 1, 0, T // 2), (BLOCKS - 1, T // 2, T)]
+        pieces = [(b, 0, T) for b in range(BLOCKS - 2)]
+        pieces += [(b, t0, t0 + T // 2) for b in range(BLOCKS - 2, BLOCKS) for t0 in (0, T // 2)]
         waiting = None
         for b, t0, t1 in pieces:
             idx = slice(t0 // 16, t1 // 16)

@@ -32,7 +32,6 @@ QUANTIZE_EXPERTS = [(0, 2), (2, 4), (4, 5), (5, 6)]
 WORD_TURNED = 4
 VECTOR_RELU_FROM = 4
 EARLY_BLOCKS = 2
-WARM_PASSES = 6
 RUN = 2 * T // P
 BLOCKS_BEFORE_SUMS = 5
 BLOCKS_ON_PAIR = (3, 4, 6, 7)
@@ -79,10 +78,6 @@ def tile_moe_cpy_mlp_relu2_kernel(
         head = FIRST_EXPERTS * PASSES
         nc.vector.memset(xs[:], 0)
         first_w2 = keep.tile([P, E, EARLY_BLOCKS * 2 * P], U8, name="first_w2", align_bytes=64)
-        warm_words = first_w2[:, :2, :].rearrange("p e c -> p (e c)")
-        nc.vector.memset(warm_words.bitcast(I32), 0)
-        nc.vector.memset(hq[:, :P].bitcast(I32), 0)
-        nc.vector.memset(hs[:, :H].bitcast(I32), 0)
         nc.gpsimd.memset(plane_a[:], 0)
         nc.gpsimd.memset(zeros[:], 0.0)
         nc.vector.memset(plane_b[:], 0)
@@ -113,18 +108,6 @@ def tile_moe_cpy_mlp_relu2_kernel(
             )
 
         big = ctx.enter_context(tc.tile_pool(name="big", bufs=1))
-
-        warm = psum.tile([P, H], F32, name="warm", tag="single", bufs=1)
-        for n in range(WARM_PASSES):
-            nc.tensor.matmul_mx(
-                out=warm[:],
-                lhsT=hq[:, :P].bitcast(FP8X4),
-                lhsT_scale=hs[:, :P],
-                rhs=warm_words.bitcast(FP4X4),
-                rhs_scale=hs[:, :H],
-                start=True,
-                stop=True,
-            )
 
         gates = keep.tile([P, 2, T], F32, name="gates", align_bytes=64)
         by_run = gates[:].rearrange("p r (n j) -> p (r n) j", j=RUN)

@@ -22,9 +22,11 @@ PASSES = K // (P * PACK)
 SLOTS = E * C
 BLOCKS = K // P
 WINDOW = SLOTS + T + PAD
-TENSOR_ADDS = 6
-WORD_PIECES = [(0, 1), (1, 2), (2, 4), (4, 5), (5, 6)]
-BYTE_PIECES = [(0, 1), (1, 2), (2, 4), (4, 6)]
+SHARED_FROM, SHARED_TO = 1, 7
+LAG = 5
+PARTS = T // P
+WORD_PIECES = [(0, 2), (2, 4), (4, 5), (5, 6)]
+BYTE_PIECES = [(0, 2), (2, 4), (4, 6)]
 W1_LOADS = [(0, 1), (1, 2), (2, 4), (4, 6)]
 FIRST_EXPERTS = 2
 W2_LOADS = [(0, 2), (2, 5), (5, 8)]
@@ -33,7 +35,6 @@ WORD_TURNED = 4
 VECTOR_RELU_FROM = 4
 EARLY_BLOCKS = 2
 RUN = 2 * T // P
-BLOCKS_BEFORE_SUMS = 5
 BLOCKS_ON_PAIR = (3, 4, 6, 7)
 
 
@@ -44,13 +45,13 @@ def tile_moe_cpy_mlp_relu2_kernel(
     with ExitStack() as ctx:
         keep = ctx.enter_context(tc.tile_pool(name="keep", bufs=1))
         ring = ctx.enter_context(tc.tile_pool(name="ring", bufs=3))
-        prods = ctx.enter_context(tc.tile_pool(name="prods", bufs=8))
+        prods = ctx.enter_context(tc.tile_pool(name="prods", bufs=6))
         psum = ctx.enter_context(tc.psum_pool(name="psum", bufs=3))
 
         offs_sb = keep.tile([P, SLOTS // 16], U16, name="offs_sb")
         pos1_sb = keep.tile([P, T // 16], U16, name="pos1_sb")
         pos2_sb = keep.tile([P, T // 16], U16, name="pos2_sb")
-        xw = [keep.tile([P, T], I32, name=f"xw{s}", align_bytes=64) for s in range(PASSES)]
+        xw = keep.tile([P, PASSES * T], I32, name="xw", align_bytes=64)
         xs = keep.tile([P, PASSES, T // 4], I32, name="xs", align_bytes=64)
         plane_a = keep.tile([P, FIRST_EXPERTS * K // 4], I32, name="plane_a", align_bytes=64)
         plane_b = keep.tile([P, E * (BLOCKS - EARLY_BLOCKS) * P // 4], I32, name="plane_b", align_bytes=64)
@@ -77,16 +78,15 @@ def tile_moe_cpy_mlp_relu2_kernel(
         w1_rows = w1_scales.rearrange("e s (q r) i -> r q (e s) i", r=4)
         head = FIRST_EXPERTS * PASSES
         nc.vector.memset(xs[:], 0)
-        first_w2 = keep.tile([P, E, EARLY_BLOCKS * 2 * P], U8, name="first_w2", align_bytes=64)
         nc.gpsimd.memset(plane_a[:], 0)
         nc.gpsimd.memset(zeros[:], 0.0)
         nc.vector.memset(plane_b[:], 0)
         nc.sync.dma_start(offs_sb[:], offs)
-        nc.sync.dma_start(xw[0][:], x_words[0].rearrange("p t d -> p (t d)").bitcast(I32))
-        gate_row = keep.tile([P, RUN], F32, name="gate_row")
+        nc.sync.dma_start(xw[:, :T], x_words[0].rearrange("p t d -> p (t d)").bitcast(I32))
+        gate_row = keep.tile([P, RUN], F32, name="gate_row", tag="gate_then_bytes", align_bytes=64)
         nc.sync.dma_start(gate_row[:], gate[:, 0, :].rearrange("r (n j) -> r n j", j=RUN))
         load_scales(xs, x_scales.rearrange("s (q r) t -> r q s t", r=4))
-        nc.sync.dma_start(xw[1][:], x_words[1].rearrange("p t d -> p (t d)").bitcast(I32))
+        nc.sync.dma_start(xw[:, T:], x_words[1].rearrange("p t d -> p (t d)").bitcast(I32))
         load_w1(keep, 0)
         load_scales(w1s_a, [w1_rows[r][:, :head, :] for r in range(4)])
         load_w1(keep, 1)
@@ -117,6 +117,12 @@ def tile_moe_cpy_mlp_relu2_kernel(
                 nc.tensor.transpose(spread[:, j, :], gate_row[:, j0 + j : j0 + j + 1].to_broadcast([P, P]), ident[:])
             nc.scalar.activation(by_run[:, :, j0 : j0 + PACK], spread[:].rearrange("p j n -> p n j"), ACT.Copy)
 
+        gate2_by_token = keep.tile([P, PARTS], F32, name="gate2_by_token")
+        upright = psum.tile([P, PARTS, P], F32, name="upright", tag="small", bufs=2)
+        for q in range(PARTS):
+            nc.tensor.transpose(upright[:, q, :], gates[:, 1, q * P : (q + 1) * P], ident[:])
+        nc.scalar.activation(gate2_by_token[:], upright[:, :, 0], ACT.Copy)
+
         def load_xr(win, b):
             nc.sync.dma_start(win[:, SLOTS : SLOTS + T], xr[b * P : (b + 1) * P, :])
 
@@ -124,33 +130,45 @@ def tile_moe_cpy_mlp_relu2_kernel(
 
         def load_w2(pool, n, tag):
             b0, b1 = W2_LOADS[n]
-            tile = pool.tile([P, E, (b1 - b0) * 2 * P], U8, name=f"w2_{n}", tag=tag, align_bytes=64) if pool else tag
+            tile = pool.tile([P, E, (b1 - b0) * 2 * P], U8, name=f"w2_{n}", tag=tag, align_bytes=64)
             src = w2_words.rearrange("e o p c -> p (e o) c")[:, :, b0 * 2 * P : b1 * 2 * P]
             nc.sync.dma_start(tile[:].bitcast(I32), src.bitcast(I32))
             w2.extend(tile[:, :, (b - b0) * 2 * P : (b - b0 + 1) * 2 * P] for b in range(b0, b1))
 
         for n in range(2, len(W1_LOADS)):
             load_w1(big, n)
-        load_w2(None, 0, first_w2)
+        load_w2(big, 0, "w2_first")
         wins = [big.tile([P, WINDOW], F32, name="win0")]
         load_xr(wins[0], 0)
         nc.scalar.activation(wins[0][:, SLOTS + T :], zeros[:], ACT.Copy)
 
-        with tc.tile_pool(name="gathered", bufs=2, side="right") as gathered:
-            words, scale_bytes = [], []
+        with tc.tile_pool(name="gathered", bufs=1, side="right") as gathered:
+            words, scale_bytes = {}, {}
+            first_bytes = gathered.tile([P, PASSES, FIRST_EXPERTS * C], U8, name="first_bytes", align_bytes=64)
+            later_bytes = keep.tile([P, PASSES, (E - FIRST_EXPERTS) * C], U8, name="later_bytes", tag="gate_then_bytes", align_bytes=64)
 
-            def gather(pieces, n, name, dtype, depth, window, found):
-                e0, e1 = pieces[n]
-                idx = offs_sb[:, e0 * C // 16 : e1 * C // 16]
-                tiles = [gathered.tile([P, (e1 - e0) * C], dtype, name=f"{name}{s}", align_bytes=64, bufs=depth) for s in range(PASSES)]
+            def gather(e0, e1, s, into, window, found):
+                nc.vector.tensor_copy(into, window.indirect(offs_sb[:, e0 * C // 16 : e1 * C // 16]))
+                for e in range(e0, e1):
+                    found[e, s] = into[:, (e - e0) * C : (e - e0 + 1) * C]
+
+            def gather_bytes(e0, e1):
                 for s in range(PASSES):
-                    nc.vector.tensor_copy(tiles[s][:], window(s).bitcast(dtype).indirect(idx))
-                found.extend([t[:, (e - e0) * C : (e - e0 + 1) * C] for t in tiles] for e in range(e0, e1))
+                    into = first_bytes[:, s, :] if e0 == 0 else later_bytes[:, s, (e0 - FIRST_EXPERTS) * C : (e1 - FIRST_EXPERTS) * C]
+                    gather(e0, e1, s, into, xs[:, s, :].bitcast(U8), scale_bytes)
 
-            for n in range(len(WORD_PIECES)):
-                if n < len(BYTE_PIECES):
-                    gather(BYTE_PIECES, n, "sg", U8, 2, lambda s: xs[:, s, :], scale_bytes)
-                gather(WORD_PIECES, n, "xg", U32, 3, lambda s: xw[s][:], words)
+            def gather_words(e0, e1, s):
+                tile = gathered.tile([P, (e1 - e0) * C], U32, name=f"xg{s}_{e0}", align_bytes=64)
+                window = xw[:, s * T : T if (e0, s) == (0, 0) else PASSES * T]
+                gather(e0, e1, s, tile[:], window.bitcast(U32), words)
+
+            gather_words(0, FIRST_EXPERTS, 0)
+            for e0, e1 in BYTE_PIECES:
+                gather_bytes(e0, e1)
+                for w0, w1_end in WORD_PIECES:
+                    if e0 <= w0 < e1:
+                        for s in range(1 if w0 == 0 else 0, PASSES):
+                            gather_words(w0, w1_end, s)
 
             def turn_and_square(e, pos):
                 cols = slice(e * C, (e + 1) * C)
@@ -182,16 +200,16 @@ def tile_moe_cpy_mlp_relu2_kernel(
                 for s in range(PASSES):
                     nc.tensor.matmul_mx(
                         out=pre[:],
-                        lhsT=words[e][s].bitcast(FP8X4),
-                        lhsT_scale=scale_bytes[e][s],
+                        lhsT=words[e, s].bitcast(FP8X4),
+                        lhsT_scale=scale_bytes[e, s],
                         rhs=w1[e][:, s, :].bitcast(FP4X4),
                         rhs_scale=(w1s_a[:, e * PASSES + s, :] if e < FIRST_EXPERTS else w1s_b[:, e * PASSES + s - head, :]).bitcast(U8),
                         start=(s == 0),
                         stop=(s == PASSES - 1),
                     )
                 pos = ring.tile([P, PACK, P], F32, name="pos", bufs=E)
-                by_place = pos[:].rearrange("p d m -> p m d")
-                sums = pre[:].rearrange("p (m d) -> p m d", d=PACK)
+                by_place = pos[:]
+                sums = pre[:].rearrange("p (m d) -> p d m", d=PACK)
                 if e == WORD_TURNED:
                     by_place = pos[:].rearrange("p d m -> p (d m)").rearrange("p (u m c) -> p u m c", u=2, c=2)
                     sums = pre[:].rearrange("p (m u c) -> p u m c", u=2, c=2)
@@ -244,48 +262,63 @@ def tile_moe_cpy_mlp_relu2_kernel(
                 else:
                     nc.scalar.activation(wins[b][:, e0 * C : e1 * C], y[:], ACT.Copy)
 
-        def add_and_store(b, t0, t1, first, second):
-            res = ring.tile([P, t1 - t0], F32, name="res", bufs=BLOCKS + 2)
-            if b < TENSOR_ADDS or (b == TENSOR_ADDS and t0 == 0):
-                parts = (t1 - t0) // P
-                total = psum.tile([P, parts, P], F32, name="total", tag="pair", bufs=2)
-                for r, term in enumerate((first, second)):
-                    for q in range(parts):
-                        nc.tensor.matmul(
-                            total[:, q, :],
-                            term[:, q * P : (q + 1) * P],
-                            ident[:],
-                            start=(r == 0 and q == 0),
-                            stop=(r == 1 and q == parts - 1),
-                            is_transpose=True,
-                        )
-                total_sb = ring.tile([P, parts, P], F32, name="total_sb")
-                nc.scalar.activation(total_sb[:], total[:], ACT.Copy)
-                back = psum.tile([P, parts, P], F32, name="back", tag="small", bufs=2)
-                for q in range(parts):
-                    nc.tensor.transpose(back[:, q, :], total_sb[:, q, :], ident[:])
-                nc.scalar.activation(res[:], back[:].rearrange("p q t -> p (q t)"), ACT.Copy)
-                nc.scalar.dma_start(out[b * P : (b + 1) * P, t0:t1], res[:])
-            else:
-                nc.vector.tensor_tensor(res[:], first[:], second[:], ALU.add)
-                nc.sync.dma_start(out[b * P : (b + 1) * P, t0:t1], res[:])
-            if b == 0:
-                for later in range(BLOCKS_BEFORE_SUMS, BLOCKS):
-                    second_layer(later)
-
-        for b in range(BLOCKS_BEFORE_SUMS):
+        for b in range(BLOCKS):
             second_layer(b)
 
-        pieces = [(b, 0, T) for b in range(BLOCKS - 2)]
-        pieces += [(b, t0, t0 + T // 2) for b in range(BLOCKS - 2, BLOCKS) for t0 in (0, T // 2)]
-        waiting = None
-        for b, t0, t1 in pieces:
-            idx = slice(t0 // 16, t1 // 16)
-            first = prods.tile([P, t1 - t0], F32, name="first")
-            nc.vector.tensor_tensor(first[:], wins[b][:].indirect(pos1_sb[:, idx]), gates[:, 0, t0:t1], ALU.mult)
-            if waiting is not None:
-                add_and_store(*waiting)
-            second = prods.tile([P, t1 - t0], F32, name="second")
-            nc.vector.tensor_tensor(second[:], wins[b][:].indirect(pos2_sb[:, idx]), gates[:, 1, t0:t1], ALU.mult)
-            waiting = (b, t0, t1, first, second)
-        add_and_store(*waiting)
+
+        def gated(b, r, lists):
+            term = prods.tile([P, T], F32, name="term")
+            nc.vector.tensor_tensor(term[:], wins[b][:].indirect(lists[:]), gates[:, r, :], ALU.mult)
+            return term
+
+        def add(b, first, seconds):
+            for t0, t1, second in seconds:
+                res = ring.tile([P, t1 - t0], F32, name="res", bufs=BLOCKS + 1)
+                nc.vector.tensor_tensor(res[:], second, first[:, t0:t1], ALU.add)
+                nc.sync.dma_start(out[b * P : (b + 1) * P, t0:t1], res[:])
+
+        def fetch_and_turn(b):
+            raw = ring.tile([P, T], F32, name="raw", bufs=2)
+            nc.scalar.activation(raw[:], wins[b][:].indirect(pos2_sb[:]), ACT.Copy)
+            turned = psum.tile([P, PARTS, P], F32, name="there", tag="pair", bufs=2)
+            for q in range(PARTS):
+                nc.tensor.transpose(turned[:, q, :], raw[:, q * P : (q + 1) * P], ident[:])
+            return turned
+
+        def scale_and_return(turned, width):
+            scaled = ring.tile([P, PARTS, P], F32, name="scaled", bufs=2)
+            found = []
+            for q0 in range(0, PARTS, width):
+                back = psum.tile([P, width, P], F32, name="back", tag="sums")
+                for q in range(q0, q0 + width):
+                    nc.scalar.activation(scaled[:, q, :], turned[:, q, :], ACT.Copy, scale=gate2_by_token[:, q : q + 1])
+                    nc.tensor.transpose(back[:, q - q0, :], scaled[:, q, :], ident[:])
+                found.append((q0 * P, (q0 + width) * P, back[:].rearrange("p q t -> p (q t)")))
+            return found
+
+        shared = list(range(SHARED_FROM, SHARED_TO))
+        backs = {}
+        turned = fetch_and_turn(shared[0])
+        for b in shared:
+            ahead = fetch_and_turn(b + 1) if b + 1 in shared else None
+            backs[b] = scale_and_return(turned, PARTS if ahead is not None else PARTS // 2)
+            turned = ahead
+
+        firsts = {}
+        waiting = []
+        for b in range(BLOCKS):
+            firsts[b] = gated(b, 0, pos1_sb)
+            if waiting:
+                add(*waiting.pop(0))
+            if b in shared:
+                if b - LAG in shared:
+                    add(b - LAG, firsts[b - LAG], backs[b - LAG])
+            else:
+                if b - LAG in shared:
+                    add(b - LAG, firsts[b - LAG], backs[b - LAG])
+                waiting.append((b, firsts[b], [(0, T, gated(b, 1, pos2_sb)[:])]))
+        rest = [b for b in shared if b + LAG >= BLOCKS]
+        add(rest[0], firsts[rest[0]], backs[rest[0]])
+        add(*waiting.pop(0))
+        for b in rest[1:]:
+            add(b, firsts[b], backs[b])

@@ -54,7 +54,8 @@ def tile_moe_cpy_mlp_relu2_kernel(
         xw = keep.tile([P, PASSES * T], I32, name="xw", align_bytes=64)
         xs = keep.tile([P, PASSES, T // 4], I32, name="xs", align_bytes=64)
         plane_a = keep.tile([P, FIRST_EXPERTS * K // 4], I32, name="plane_a", align_bytes=64)
-        plane_b = keep.tile([P, E * (BLOCKS - EARLY_BLOCKS) * P // 4], I32, name="plane_b", align_bytes=64)
+        plane_b = keep.tile([P, (E - FIRST_EXPERTS) * K // 4], I32, name="plane_b", align_bytes=64)
+        plane_c = keep.tile([P, E * (BLOCKS - EARLY_BLOCKS) * P // 4], I32, name="plane_c", align_bytes=64)
         ident = keep.tile([P, P], F32, name="ident")
         zeros = keep.tile([P, PAD], F32, name="zeros")
         hb = keep.tile([P, SLOTS, PACK], BF16, name="hb", align_bytes=64)
@@ -107,6 +108,7 @@ def tile_moe_cpy_mlp_relu2_kernel(
                 channel_multiplier=1,
             )
 
+        nc.vector.memset(plane_c[:], 0)
         big = ctx.enter_context(tc.tile_pool(name="big", bufs=1))
 
         gates = keep.tile([P, 2, T], F32, name="gates", align_bytes=64)
@@ -224,11 +226,11 @@ def tile_moe_cpy_mlp_relu2_kernel(
         w2_rows = w2_scales.rearrange("e o (q r) n -> r q (e o) n", r=4)
         cut = EARLY_BLOCKS * P
         early = plane_a[:, : E * cut // 4].rearrange("p (e n) -> p e n", e=E)
-        rest = plane_b[:].rearrange("p (e n) -> p e n", e=E)
+        rest = plane_c[:].rearrange("p (e n) -> p e n", e=E)
         load_scales(early, [w2_rows[r][:, :, :cut] for r in range(4)])
+        load_scales(rest, [w2_rows[r][:, :, cut:] for r in range(4)])
         load_w2(big, 1, "slot2")
         late = ctx.enter_context(tc.tile_pool(name="late", bufs=1, side="right"))
-        load_scales(rest, [w2_rows[r][:, :, cut:] for r in range(4)])
         for b in range(1, BLOCKS):
             wins.append(late.tile([P, WINDOW], F32, name=f"win{b}"))
             load_xr(wins[b], b)

@@ -33,7 +33,6 @@ W2_LOADS = [(0, 2), (2, 5), (5, 8)]
 QUANTIZE_EXPERTS = [(0, 2), (2, 4), (4, 5), (5, 6)]
 WORD_TURNED = 4
 VECTOR_RELU_FROM = 4
-EARLY_BLOCKS = 2
 RUN = 2 * T // P
 BLOCKS_ON_PAIR = (3, 4, 6, 7)
 
@@ -55,7 +54,7 @@ def tile_moe_cpy_mlp_relu2_kernel(
         xs = keep.tile([P, PASSES, T // 4], I32, name="xs", align_bytes=64)
         plane_a = keep.tile([P, FIRST_EXPERTS * K // 4], I32, name="plane_a", align_bytes=64)
         plane_b = keep.tile([P, (E - FIRST_EXPERTS) * K // 4], I32, name="plane_b", align_bytes=64)
-        plane_c = keep.tile([P, E * (BLOCKS - EARLY_BLOCKS) * P // 4], I32, name="plane_c", align_bytes=64)
+        plane_c = keep.tile([P, E * K // 4], I32, name="plane_c", align_bytes=64)
         ident = keep.tile([P, P], F32, name="ident")
         zeros = keep.tile([P, PAD], F32, name="zeros")
         hb = keep.tile([P, SLOTS, PACK], BF16, name="hb", align_bytes=64)
@@ -92,8 +91,6 @@ def tile_moe_cpy_mlp_relu2_kernel(
         load_scales(w1s_a, [w1_rows[r][:, :head, :] for r in range(4)])
         load_w1(keep, 1)
         load_scales(w1s_b, [w1_rows[r][:, head:, :] for r in range(4)])
-        nc.sync.dma_start(pos1_sb[:], pos1)
-        nc.sync.dma_start(pos2_sb[:], pos2)
 
         with tc.tile_pool(name="setup", bufs=1) as setup:
             blank = setup.tile([P, P], F32, name="blank")
@@ -108,7 +105,10 @@ def tile_moe_cpy_mlp_relu2_kernel(
                 channel_multiplier=1,
             )
 
-        nc.vector.memset(plane_c[:], 0)
+        zero_words = keep.tile([P, H], I32, name="zero_words")
+        nc.vector.memset(zero_words[:], 0)
+        for c0 in range(0, E * K // 4, H):
+            nc.scalar.copy(plane_c[:, c0 : c0 + H].bitcast(U32), zero_words[:].bitcast(U32))
         big = ctx.enter_context(tc.tile_pool(name="big", bufs=1))
 
         gates = keep.tile([P, 2, T], F32, name="gates", align_bytes=64)
@@ -139,10 +139,17 @@ def tile_moe_cpy_mlp_relu2_kernel(
 
         for n in range(2, len(W1_LOADS)):
             load_w1(big, n)
-        load_w2(big, 0, "w2_first")
-        wins = [big.tile([P, WINDOW], F32, name="win0")]
-        load_xr(wins[0], 0)
-        nc.scalar.activation(wins[0][:, SLOTS + T :], zeros[:], ACT.Copy)
+        w2_planes = plane_c[:].rearrange("p (e n) -> p e n", e=E)
+        load_scales(w2_planes, w2_scales.rearrange("e o (q r) n -> r q (e o) n", r=4))
+        wins = [big.tile([P, WINDOW], F32, name=f"win{b}") for b in range(BLOCKS)]
+        for b in range(BLOCKS):
+            if b < len(W2_LOADS):
+                load_w2(big, b, f"w2_{b}")
+            load_xr(wins[b], b)
+            if b == 0:
+                nc.sync.dma_start(pos1_sb[:], pos1)
+                nc.sync.dma_start(pos2_sb[:], pos2)
+            nc.scalar.activation(wins[b][:, SLOTS + T :], zeros[:], ACT.Copy)
 
         with tc.tile_pool(name="gathered", bufs=1, side="right") as gathered:
             words, scale_bytes = {}, {}
@@ -223,26 +230,6 @@ def tile_moe_cpy_mlp_relu2_kernel(
                 for done in turns_after.get(e, ()):
                     turn_and_square(done, positive[done])
 
-        w2_rows = w2_scales.rearrange("e o (q r) n -> r q (e o) n", r=4)
-        cut = EARLY_BLOCKS * P
-        early = plane_a[:, : E * cut // 4].rearrange("p (e n) -> p e n", e=E)
-        rest = plane_c[:].rearrange("p (e n) -> p e n", e=E)
-        load_scales(early, [w2_rows[r][:, :, :cut] for r in range(4)])
-        load_scales(rest, [w2_rows[r][:, :, cut:] for r in range(4)])
-        load_w2(big, 1, "slot2")
-        late = ctx.enter_context(tc.tile_pool(name="late", bufs=1, side="right"))
-        for b in range(1, BLOCKS):
-            wins.append(late.tile([P, WINDOW], F32, name=f"win{b}"))
-            load_xr(wins[b], b)
-            nc.gpsimd.memset(wins[b][:, SLOTS + T :], 0.0)
-            if b == 1:
-                load_w2(late, 2, "w2_last")
-
-        def w2_scale(e, b):
-            if b < EARLY_BLOCKS:
-                return early[:, e, b * P // 4 : (b + 1) * P // 4].bitcast(U8)
-            return rest[:, e, (b - EARLY_BLOCKS) * P // 4 : (b - EARLY_BLOCKS + 1) * P // 4].bitcast(U8)
-
         def second_layer(b):
             wide = ("sums", 0, 4, 3) if b not in BLOCKS_ON_PAIR else ("pair", 0, 4, 2)
             narrow = [("small", 4, 5, 2), ("small", 5, E, 2)] if b == 0 else [("small", 4, E, 2)]
@@ -253,7 +240,7 @@ def tile_moe_cpy_mlp_relu2_kernel(
                     nc.tensor.matmul_mx(
                         out=y[:, (e - e0) * C : (e - e0 + 1) * C],
                         lhsT=w2[b][:, e, :].bitcast(FP4X4),
-                        lhsT_scale=w2_scale(e, b),
+                        lhsT_scale=w2_planes[:, e, b * P // 4 : (b + 1) * P // 4].bitcast(U8),
                         rhs=hq[:, cols].bitcast(FP8X4),
                         rhs_scale=hs[:, cols],
                         start=True,

@@ -21,20 +21,26 @@ PACK = 4
 PASSES = K // (P * PACK)
 SLOTS = E * C
 BLOCKS = K // P
+PARTS = T // P
 WINDOW = SLOTS + T + PAD
+RUN = 2 * T // P
+
+FIRST_EXPERTS = 2
+W1_LOADS = [(0, 1), (1, 2), (2, 4), (4, 6)]
+BYTE_PIECES = [(0, 2), (2, 4), (4, 6)]
+WORD_PIECES = [(0, 2), (2, 4), (4, 5), (5, 6)]
+VECTOR_RELU_FROM = 4
+WORD_TURNED = 4
+TURNS_AFTER = {1: (0, 1), 5: (2, 3, 5, 4)}
+QUANTIZE_EXPERTS = [(0, 2), (2, 3), (3, 4), (4, 5), (5, 6)]
+EARLY_BLOCKS = 4
+EARLY_AFTER_TURN = 3
+W2_LOADS = [(0, 2, 0, 4), (2, 6, 0, 2), (2, 6, 2, 4), (0, 6, 4, 8)]
+WIDE_EXPERTS = 4
 SHARED_FROM, SHARED_TO = 1, 7
 LAG = 5
-PARTS = T // P
-WORD_PIECES = [(0, 2), (2, 4), (4, 5), (5, 6)]
-BYTE_PIECES = [(0, 2), (2, 4), (4, 6)]
-W1_LOADS = [(0, 1), (1, 2), (2, 4), (4, 6)]
-FIRST_EXPERTS = 2
-W2_LOADS = [(0, 2), (2, 5), (5, 8)]
-QUANTIZE_EXPERTS = [(0, 2), (2, 4), (4, 5), (5, 6)]
-WORD_TURNED = 4
-VECTOR_RELU_FROM = 4
-RUN = 2 * T // P
-BLOCKS_ON_PAIR = (3, 4, 6, 7)
+LAST_CUTS = [(0, 2), (2, 3), (3, 4)]
+BACK_BANKS = 4
 
 
 def tile_moe_cpy_mlp_relu2_kernel(
@@ -44,17 +50,17 @@ def tile_moe_cpy_mlp_relu2_kernel(
     with ExitStack() as ctx:
         keep = ctx.enter_context(tc.tile_pool(name="keep", bufs=1))
         ring = ctx.enter_context(tc.tile_pool(name="ring", bufs=3))
-        prods = ctx.enter_context(tc.tile_pool(name="prods", bufs=6))
+        prods = ctx.enter_context(tc.tile_pool(name="prods", bufs=LAG + 1))
         psum = ctx.enter_context(tc.psum_pool(name="psum", bufs=3))
 
         offs_sb = keep.tile([P, SLOTS // 16], U16, name="offs_sb")
         pos1_sb = keep.tile([P, T // 16], U16, name="pos1_sb")
         pos2_sb = keep.tile([P, T // 16], U16, name="pos2_sb")
         xw = keep.tile([P, PASSES * T], I32, name="xw", align_bytes=64)
-        xs = keep.tile([P, PASSES, T // 4], I32, name="xs", align_bytes=64)
-        plane_a = keep.tile([P, FIRST_EXPERTS * K // 4], I32, name="plane_a", align_bytes=64)
-        plane_b = keep.tile([P, (E - FIRST_EXPERTS) * K // 4], I32, name="plane_b", align_bytes=64)
-        plane_c = keep.tile([P, E * K // 4], I32, name="plane_c", align_bytes=64)
+        xs = keep.tile([P, PASSES, T // PACK], I32, name="xs", align_bytes=64)
+        plane_a = keep.tile([P, FIRST_EXPERTS * K // PACK], I32, name="plane_a", align_bytes=64)
+        plane_b = keep.tile([P, (E - FIRST_EXPERTS) * K // PACK], I32, name="plane_b", align_bytes=64)
+        plane_c = keep.tile([P, E * K // PACK], I32, name="plane_c", align_bytes=64)
         ident = keep.tile([P, P], F32, name="ident")
         zeros = keep.tile([P, PAD], F32, name="zeros")
         hb = keep.tile([P, SLOTS, PACK], BF16, name="hb", align_bytes=64)
@@ -73,10 +79,10 @@ def tile_moe_cpy_mlp_relu2_kernel(
             nc.sync.dma_start(tile[:].bitcast(I32), w1_words[e0:e1].rearrange("e s p c -> p (e s) c").bitcast(I32))
             w1.extend(tile[:, (e - e0) * PASSES : (e - e0 + 1) * PASSES, :] for e in range(e0, e1))
 
-        w1s_a = plane_a[:].rearrange("p (g i) -> p g i", i=H // 4)
-        w1s_b = plane_b[:, : (E - FIRST_EXPERTS) * K // 4].rearrange("p (g i) -> p g i", i=H // 4)
+        w1s_a = plane_a[:].rearrange("p (g i) -> p g i", i=H // PACK)
+        w1s_b = plane_b[:].rearrange("p (g i) -> p g i", i=H // PACK)
         w1_rows = w1_scales.rearrange("e s (q r) i -> r q (e s) i", r=4)
-        head = FIRST_EXPERTS * PASSES
+        first_planes = FIRST_EXPERTS * PASSES
         nc.vector.memset(xs[:], 0)
         nc.gpsimd.memset(plane_a[:], 0)
         nc.gpsimd.memset(zeros[:], 0.0)
@@ -88,9 +94,9 @@ def tile_moe_cpy_mlp_relu2_kernel(
         load_scales(xs, x_scales.rearrange("s (q r) t -> r q s t", r=4))
         nc.sync.dma_start(xw[:, T:], x_words[1].rearrange("p t d -> p (t d)").bitcast(I32))
         load_w1(keep, 0)
-        load_scales(w1s_a, [w1_rows[r][:, :head, :] for r in range(4)])
+        load_scales(w1s_a, [w1_rows[r][:, :first_planes, :] for r in range(4)])
         load_w1(keep, 1)
-        load_scales(w1s_b, [w1_rows[r][:, head:, :] for r in range(4)])
+        load_scales(w1s_b, [w1_rows[r][:, first_planes:, :] for r in range(4)])
 
         with tc.tile_pool(name="setup", bufs=1) as setup:
             blank = setup.tile([P, P], F32, name="blank")
@@ -107,7 +113,7 @@ def tile_moe_cpy_mlp_relu2_kernel(
 
         zero_words = keep.tile([P, H], I32, name="zero_words")
         nc.vector.memset(zero_words[:], 0)
-        for c0 in range(0, E * K // 4, H):
+        for c0 in range(0, E * K // PACK, H):
             nc.scalar.copy(plane_c[:, c0 : c0 + H].bitcast(U32), zero_words[:].bitcast(U32))
         big = ctx.enter_context(tc.tile_pool(name="big", bufs=1))
 
@@ -125,27 +131,27 @@ def tile_moe_cpy_mlp_relu2_kernel(
             nc.tensor.transpose(upright[:, q, :], gates[:, 1, q * P : (q + 1) * P], ident[:])
         nc.scalar.activation(gate2_by_token[:], upright[:, :, 0], ACT.Copy)
 
-        def load_xr(win, b):
-            nc.sync.dma_start(win[:, SLOTS : SLOTS + T], xr[b * P : (b + 1) * P, :])
+        w2 = {}
 
-        w2 = []
-
-        def load_w2(pool, n, tag):
-            b0, b1 = W2_LOADS[n]
-            tile = pool.tile([P, E, (b1 - b0) * 2 * P], U8, name=f"w2_{n}", tag=tag, align_bytes=64)
-            src = w2_words.rearrange("e o p c -> p (e o) c")[:, :, b0 * 2 * P : b1 * 2 * P]
+        def load_w2(n):
+            e0, e1, b0, b1 = W2_LOADS[n]
+            tile = big.tile([P, e1 - e0, (b1 - b0) * 2 * P], U8, name=f"w2_{n}", align_bytes=64)
+            src = w2_words[e0:e1].rearrange("e o p c -> p (e o) c")[:, :, b0 * 2 * P : b1 * 2 * P]
             nc.sync.dma_start(tile[:].bitcast(I32), src.bitcast(I32))
-            w2.extend(tile[:, :, (b - b0) * 2 * P : (b - b0 + 1) * 2 * P] for b in range(b0, b1))
+            for e in range(e0, e1):
+                for b in range(b0, b1):
+                    w2[b, e] = tile[:, e - e0, (b - b0) * 2 * P : (b - b0 + 1) * 2 * P]
 
-        for n in range(2, len(W1_LOADS)):
+        for n in range(FIRST_EXPERTS, len(W1_LOADS)):
             load_w1(big, n)
         w2_planes = plane_c[:].rearrange("p (e n) -> p e n", e=E)
         load_scales(w2_planes, w2_scales.rearrange("e o (q r) n -> r q (e o) n", r=4))
         wins = [big.tile([P, WINDOW], F32, name=f"win{b}") for b in range(BLOCKS)]
+        load_w2(0)
         for b in range(BLOCKS):
-            if b < len(W2_LOADS):
-                load_w2(big, b, f"w2_{b}")
-            load_xr(wins[b], b)
+            if b + 1 < len(W2_LOADS):
+                load_w2(b + 1)
+            nc.sync.dma_start(wins[b][:, SLOTS : SLOTS + T], xr[b * P : (b + 1) * P, :])
             if b == 0:
                 nc.sync.dma_start(pos1_sb[:], pos1)
                 nc.sync.dma_start(pos2_sb[:], pos2)
@@ -174,79 +180,101 @@ def tile_moe_cpy_mlp_relu2_kernel(
             gather_words(0, FIRST_EXPERTS, 0)
             for e0, e1 in BYTE_PIECES:
                 gather_bytes(e0, e1)
-                for w0, w1_end in WORD_PIECES:
-                    if e0 <= w0 < e1:
-                        for s in range(1 if w0 == 0 else 0, PASSES):
-                            gather_words(w0, w1_end, s)
+                for first_expert, end_expert in WORD_PIECES:
+                    if e0 <= first_expert < e1:
+                        for s in range(1 if first_expert == 0 else 0, PASSES):
+                            gather_words(first_expert, end_expert, s)
 
-            def turn_and_square(e, pos):
+            def expert_product(into, b, e):
+                cols = slice(e * C, (e + 1) * C)
+                nc.tensor.matmul_mx(
+                    out=into,
+                    lhsT=w2[b, e].bitcast(FP4X4),
+                    lhsT_scale=w2_planes[:, e, b * P // PACK : (b + 1) * P // PACK].bitcast(U8),
+                    rhs=hq[:, cols].bitcast(FP8X4),
+                    rhs_scale=hs[:, cols],
+                    start=True,
+                    stop=True,
+                )
+
+            early = []
+
+            def early_products():
+                for b0 in range(0, EARLY_BLOCKS, 2):
+                    y = psum.tile([P, 2, FIRST_EXPERTS * C], F32, name="early_y", tag="sums")
+                    for j in range(2):
+                        for e in range(FIRST_EXPERTS):
+                            expert_product(y[:, j, e * C : (e + 1) * C], b0 + j, e)
+                        early.append(y[:, j, :])
+
+            squared = set()
+
+            def turn_and_square(e, relu):
                 cols = slice(e * C, (e + 1) * C)
                 turned = psum.tile([P, PACK, C], F32, name="turned", tag="pair" if e % 3 else "single", bufs=2 if e % 3 else 1)
                 if e == WORD_TURNED:
                     h = ring.tile([P, 2, 2 * P], BF16, name="h", bufs=1)
-                    flat = pos[:].rearrange("p (u a) m -> p u (a m)", u=2)
+                    flat = relu[:].rearrange("p (u a) m -> p u (a m)", u=2)
                     nc.vector.tensor_tensor(h[:], flat, flat, ALU.mult)
                     for u in range(2):
                         nc.tensor.transpose(turned[:, u, :], h[:, u, :].bitcast(F32), ident[:])
                     nc.vector.tensor_copy(hb[:, cols, :].bitcast(F32), turned[:, :2, :].rearrange("p u s -> p s u"))
                 else:
                     for d in range(PACK):
-                        nc.tensor.transpose(turned[:, d, :], pos[:, d, :], ident[:])
+                        nc.tensor.transpose(turned[:, d, :], relu[:, d, :], ident[:])
                     nc.scalar.activation(hb[:, cols, :], turned[:].rearrange("p d s -> p s d"), ACT.Square)
+                squared.add(e)
                 for e0, e1 in QUANTIZE_EXPERTS:
-                    if e1 == e + 1:
-                        done = slice(e0 * C, e1 * C)
+                    if e0 <= e < e1 and all(other in squared for other in range(e0, e1)):
+                        ready = slice(e0 * C, e1 * C)
                         nc.vector.quantize_mx(
-                            out=hq[:, done].bitcast(FP8X4),
-                            scales=hs[:, done],
-                            in_=hb[:, done, :].rearrange("p u j -> p (u j)"),
+                            out=hq[:, ready].bitcast(FP8X4),
+                            scales=hs[:, ready],
+                            in_=hb[:, ready, :].rearrange("p u j -> p (u j)"),
                         )
 
-            positive = []
-            turns_after = {1: (0, 1), 5: (2, 3, 5, 4)}
+            relus = []
             for e in range(E):
                 pre = psum.tile([P, H], F32, name="pre", tag="sums")
                 for s in range(PASSES):
+                    plane = w1s_a[:, e * PASSES + s, :] if e < FIRST_EXPERTS else w1s_b[:, e * PASSES + s - first_planes, :]
                     nc.tensor.matmul_mx(
                         out=pre[:],
                         lhsT=words[e, s].bitcast(FP8X4),
                         lhsT_scale=scale_bytes[e, s],
                         rhs=w1[e][:, s, :].bitcast(FP4X4),
-                        rhs_scale=(w1s_a[:, e * PASSES + s, :] if e < FIRST_EXPERTS else w1s_b[:, e * PASSES + s - head, :]).bitcast(U8),
+                        rhs_scale=plane.bitcast(U8),
                         start=(s == 0),
                         stop=(s == PASSES - 1),
                     )
-                pos = ring.tile([P, PACK, P], F32, name="pos", bufs=E)
-                by_place = pos[:]
+                relu = ring.tile([P, PACK, P], F32, name="relu", bufs=E)
+                by_place = relu[:]
                 sums = pre[:].rearrange("p (m d) -> p d m", d=PACK)
                 if e == WORD_TURNED:
-                    by_place = pos[:].rearrange("p d m -> p (d m)").rearrange("p (u m c) -> p u m c", u=2, c=2)
+                    by_place = relu[:].rearrange("p d m -> p (d m)").rearrange("p (u m c) -> p u m c", u=2, c=2)
                     sums = pre[:].rearrange("p (m u c) -> p u m c", u=2, c=2)
                 if e < VECTOR_RELU_FROM:
                     nc.scalar.activation(by_place, sums, ACT.Relu)
                 else:
                     nc.vector.tensor_scalar_max(by_place, sums, 0.0)
-                positive.append(pos)
-                for done in turns_after.get(e, ()):
-                    turn_and_square(done, positive[done])
+                relus.append(relu)
+                for due in TURNS_AFTER.get(e, ()):
+                    turn_and_square(due, relus[due])
+                    if due == EARLY_AFTER_TURN:
+                        early_products()
 
         def second_layer(b):
-            wide = ("sums", 0, 4, 3) if b not in BLOCKS_ON_PAIR else ("pair", 0, 4, 2)
-            narrow = [("small", 4, 5, 2), ("small", 5, E, 2)] if b == 0 else [("small", 4, E, 2)]
-            for tag, e0, e1, depth in [wide] + narrow:
-                y = psum.tile([P, (e1 - e0) * C], F32, name="y", tag=tag, bufs=depth)
+            groups = [("pair", 0, WIDE_EXPERTS), ("small", WIDE_EXPERTS, E)]
+            if b < EARLY_BLOCKS:
+                nc.scalar.activation(wins[b][:, : FIRST_EXPERTS * C], early[b], ACT.Copy)
+                groups = [("pair", FIRST_EXPERTS, E)]
+            if b == 0:
+                groups = [("pair", FIRST_EXPERTS, WIDE_EXPERTS)] + [("small", e, e + 1) for e in range(WIDE_EXPERTS, E)]
+            for tag, e0, e1 in groups:
+                y = psum.tile([P, (e1 - e0) * C], F32, name="y", tag=tag, bufs=2)
                 for e in range(e0, e1):
-                    cols = slice(e * C, (e + 1) * C)
-                    nc.tensor.matmul_mx(
-                        out=y[:, (e - e0) * C : (e - e0 + 1) * C],
-                        lhsT=w2[b][:, e, :].bitcast(FP4X4),
-                        lhsT_scale=w2_planes[:, e, b * P // 4 : (b + 1) * P // 4].bitcast(U8),
-                        rhs=hq[:, cols].bitcast(FP8X4),
-                        rhs_scale=hs[:, cols],
-                        start=True,
-                        stop=True,
-                    )
-                if b == 0 and e0 > 0:
+                    expert_product(y[:, (e - e0) * C : (e - e0 + 1) * C], b, e)
+                if b == 0 and e0 >= WIDE_EXPERTS:
                     nc.vector.tensor_copy(wins[b][:, e0 * C : e1 * C], y[:])
                 else:
                     nc.scalar.activation(wins[b][:, e0 * C : e1 * C], y[:], ACT.Copy)
@@ -254,60 +282,60 @@ def tile_moe_cpy_mlp_relu2_kernel(
         for b in range(BLOCKS):
             second_layer(b)
 
-
-        def gated(b, r, lists):
+        def gated(b, r, positions):
             term = prods.tile([P, T], F32, name="term")
-            nc.vector.tensor_tensor(term[:], wins[b][:].indirect(lists[:]), gates[:, r, :], ALU.mult)
+            nc.vector.tensor_tensor(term[:], wins[b][:].indirect(positions[:]), gates[:, r, :], ALU.mult)
             return term
 
-        def add(b, first, seconds):
+        def add_and_store(b, first, seconds):
             for t0, t1, second in seconds:
-                res = ring.tile([P, t1 - t0], F32, name="res", bufs=BLOCKS + 1)
+                res = ring.tile([P, t1 - t0], F32, name="res", bufs=BLOCKS + len(LAST_CUTS) - 1)
                 nc.vector.tensor_tensor(res[:], second, first[:, t0:t1], ALU.add)
                 nc.sync.dma_start(out[b * P : (b + 1) * P, t0:t1], res[:])
 
         def fetch_and_turn(b):
             raw = ring.tile([P, T], F32, name="raw", bufs=2)
             nc.scalar.activation(raw[:], wins[b][:].indirect(pos2_sb[:]), ACT.Copy)
-            turned = psum.tile([P, PARTS, P], F32, name="there", tag="pair", bufs=2)
+            there = psum.tile([P, PARTS, P], F32, name="there", tag="pair", bufs=2)
             for q in range(PARTS):
-                nc.tensor.transpose(turned[:, q, :], raw[:, q * P : (q + 1) * P], ident[:])
-            return turned
+                nc.tensor.transpose(there[:, q, :], raw[:, q * P : (q + 1) * P], ident[:])
+            return there
 
-        def scale_and_return(turned, width):
+        returned = []
+
+        def scale_and_return(there, cuts):
             scaled = ring.tile([P, PARTS, P], F32, name="scaled", bufs=2)
-            found = []
-            for q0 in range(0, PARTS, width):
-                back = psum.tile([P, width, P], F32, name="back", tag="sums")
-                for q in range(q0, q0 + width):
-                    nc.scalar.activation(scaled[:, q, :], turned[:, q, :], ACT.Copy, scale=gate2_by_token[:, q : q + 1])
+            pieces = []
+            for q0, q1 in cuts:
+                spare = len(returned) % BACK_BANKS == BACK_BANKS - 1
+                back = psum.tile([P, q1 - q0, P], F32, name="back", tag="single" if spare else "sums", bufs=1 if spare else 3)
+                returned.append(back)
+                for q in range(q0, q1):
+                    nc.scalar.activation(scaled[:, q, :], there[:, q, :], ACT.Copy, scale=gate2_by_token[:, q : q + 1])
                     nc.tensor.transpose(back[:, q - q0, :], scaled[:, q, :], ident[:])
-                found.append((q0 * P, (q0 + width) * P, back[:].rearrange("p q t -> p (q t)")))
-            return found
+                pieces.append((q0 * P, q1 * P, back[:].rearrange("p q t -> p (q t)")))
+            return pieces
 
         shared = list(range(SHARED_FROM, SHARED_TO))
         backs = {}
-        turned = fetch_and_turn(shared[0])
+        there = fetch_and_turn(shared[0])
         for b in shared:
             ahead = fetch_and_turn(b + 1) if b + 1 in shared else None
-            backs[b] = scale_and_return(turned, PARTS if ahead is not None else PARTS // 2)
-            turned = ahead
+            backs[b] = scale_and_return(there, [(0, PARTS)] if ahead is not None else LAST_CUTS)
+            there = ahead
 
         firsts = {}
         waiting = []
         for b in range(BLOCKS):
             firsts[b] = gated(b, 0, pos1_sb)
             if waiting:
-                add(*waiting.pop(0))
-            if b in shared:
-                if b - LAG in shared:
-                    add(b - LAG, firsts[b - LAG], backs[b - LAG])
-            else:
-                if b - LAG in shared:
-                    add(b - LAG, firsts[b - LAG], backs[b - LAG])
+                add_and_store(*waiting.pop(0))
+            if b - LAG in shared:
+                add_and_store(b - LAG, firsts[b - LAG], backs[b - LAG])
+            if b not in shared:
                 waiting.append((b, firsts[b], [(0, T, gated(b, 1, pos2_sb)[:])]))
-        rest = [b for b in shared if b + LAG >= BLOCKS]
-        add(rest[0], firsts[rest[0]], backs[rest[0]])
-        add(*waiting.pop(0))
-        for b in rest[1:]:
-            add(b, firsts[b], backs[b])
+        left = [b for b in shared if b + LAG >= BLOCKS]
+        add_and_store(left[0], firsts[left[0]], backs[left[0]])
+        add_and_store(*waiting.pop(0))
+        for b in left[1:]:
+            add_and_store(b, firsts[b], backs[b])

@@ -35,7 +35,7 @@ TURNS_AFTER = {1: (0, 1), 5: (2, 3, 5, 4)}
 QUANTIZE_EXPERTS = [(0, 2), (2, 3), (3, 4), (4, 5), (5, 6)]
 EARLY_BLOCKS = 4
 EARLY_AFTER_TURN = 3
-W2_LOADS = [(0, 2, 0, 4), (2, 6, 0, 2), (2, 6, 2, 4), (0, 6, 4, 8)]
+W2_LOADS = [(0, 2, 0, 4), (2, 6, 0, 4), (0, 6, 4, 8)]
 WIDE_EXPERTS = 4
 SHARED_FROM, SHARED_TO = 1, 7
 LAG = 5
@@ -148,13 +148,13 @@ def tile_moe_cpy_mlp_relu2_kernel(
         load_scales(w2_planes, w2_scales.rearrange("e o (q r) n -> r q (e o) n", r=4))
         wins = [big.tile([P, WINDOW], F32, name=f"win{b}") for b in range(BLOCKS)]
         load_w2(0)
+        load_w2(1)
         for b in range(BLOCKS):
-            if b + 1 < len(W2_LOADS):
-                load_w2(b + 1)
             nc.sync.dma_start(wins[b][:, SLOTS : SLOTS + T], xr[b * P : (b + 1) * P, :])
             if b == 0:
                 nc.sync.dma_start(pos1_sb[:], pos1)
                 nc.sync.dma_start(pos2_sb[:], pos2)
+                load_w2(2)
             nc.scalar.activation(wins[b][:, SLOTS + T :], zeros[:], ACT.Copy)
 
         with tc.tile_pool(name="gathered", bufs=1, side="right") as gathered:
@@ -271,7 +271,9 @@ def tile_moe_cpy_mlp_relu2_kernel(
             if b == 0:
                 groups = [("pair", FIRST_EXPERTS, WIDE_EXPERTS)] + [("small", e, e + 1) for e in range(WIDE_EXPERTS, E)]
             for tag, e0, e1 in groups:
-                y = psum.tile([P, (e1 - e0) * C], F32, name="y", tag=tag, bufs=2)
+                if tag == "pair" and b % 2:
+                    tag = "sums"
+                y = psum.tile([P, (e1 - e0) * C], F32, name="y", tag=tag, bufs=3 if tag == "sums" else 2)
                 for e in range(e0, e1):
                     expert_product(y[:, (e - e0) * C : (e - e0 + 1) * C], b, e)
                 if b == 0 and e0 >= WIDE_EXPERTS:

@@ -23,7 +23,6 @@ SLOTS = E * C
 BLOCKS = K // P
 PARTS = T // P
 WINDOW = SLOTS + T + PAD
-RUN = 2 * T // P
 
 FIRST_EXPERTS = 2
 W1_LOADS = [(0, 1), (1, 2), (2, 4), (4, 6)]
@@ -38,7 +37,7 @@ EARLY_AFTER_TURN = 3
 W2_LOADS = [(0, 2, 0, 4), (2, 6, 0, 4), (0, 6, 4, 8)]
 WIDE_EXPERTS = 4
 SHARED_FROM, SHARED_TO = 1, 7
-LAG = 5
+LAG = 4
 LAST_CUTS = [(0, 2), (2, 3), (3, 4)]
 BACK_BANKS = 4
 
@@ -50,7 +49,7 @@ def tile_moe_cpy_mlp_relu2_kernel(
     with ExitStack() as ctx:
         keep = ctx.enter_context(tc.tile_pool(name="keep", bufs=1))
         ring = ctx.enter_context(tc.tile_pool(name="ring", bufs=3))
-        prods = ctx.enter_context(tc.tile_pool(name="prods", bufs=LAG + 1))
+        prods = ctx.enter_context(tc.tile_pool(name="prods", bufs=1))
         psum = ctx.enter_context(tc.psum_pool(name="psum", bufs=3))
 
         offs_sb = keep.tile([P, SLOTS // 16], U16, name="offs_sb")
@@ -62,7 +61,6 @@ def tile_moe_cpy_mlp_relu2_kernel(
         plane_b = keep.tile([P, (E - FIRST_EXPERTS) * K // PACK], I32, name="plane_b", align_bytes=64)
         plane_c = keep.tile([P, E * K // PACK], I32, name="plane_c", align_bytes=64)
         ident = keep.tile([P, P], F32, name="ident")
-        zeros = keep.tile([P, PAD], F32, name="zeros")
         hb = keep.tile([P, SLOTS, PACK], BF16, name="hb", align_bytes=64)
         hq = keep.tile([P, SLOTS], U32, name="hq", align_bytes=64)
         hs = keep.tile([P, SLOTS], U8, name="hs", align_bytes=64)
@@ -84,13 +82,13 @@ def tile_moe_cpy_mlp_relu2_kernel(
         w1_rows = w1_scales.rearrange("e s (q r) i -> r q (e s) i", r=4)
         first_planes = FIRST_EXPERTS * PASSES
         nc.vector.memset(xs[:], 0)
+        gate_rows = keep.tile([P, P], F32, name="gate_rows")
+        nc.gpsimd.memset(gate_rows[:], 0.0)
         nc.gpsimd.memset(plane_a[:], 0)
-        nc.gpsimd.memset(zeros[:], 0.0)
         nc.vector.memset(plane_b[:], 0)
         nc.sync.dma_start(offs_sb[:], offs)
         nc.sync.dma_start(xw[:, :T], x_words[0].rearrange("p t d -> p (t d)").bitcast(I32))
-        gate_row = keep.tile([P, RUN], F32, name="gate_row", tag="gate_then_bytes", align_bytes=64)
-        nc.sync.dma_start(gate_row[:], gate[:, 0, :].rearrange("r (n j) -> r n j", j=RUN))
+        nc.sync.dma_start(gate_rows[: 2 * PARTS, :], gate[:, 0, :].rearrange("r (q n) -> r q n", n=P))
         load_scales(xs, x_scales.rearrange("s (q r) t -> r q s t", r=4))
         nc.sync.dma_start(xw[:, T:], x_words[1].rearrange("p t d -> p (t d)").bitcast(I32))
         load_w1(keep, 0)
@@ -117,19 +115,20 @@ def tile_moe_cpy_mlp_relu2_kernel(
             nc.scalar.copy(plane_c[:, c0 : c0 + H].bitcast(U32), zero_words[:].bitcast(U32))
         big = ctx.enter_context(tc.tile_pool(name="big", bufs=1))
 
-        gates = keep.tile([P, 2, T], F32, name="gates", align_bytes=64)
-        by_run = gates[:].rearrange("p r (n j) -> p (r n) j", j=RUN)
-        for j0 in range(0, RUN, PACK):
-            spread = psum.tile([P, PACK, P], F32, name="spread", tag="pair" if j0 else "single", bufs=2 if j0 else 1)
-            for j in range(PACK):
-                nc.tensor.transpose(spread[:, j, :], gate_row[:, j0 + j : j0 + j + 1].to_broadcast([P, P]), ident[:])
-            nc.scalar.activation(by_run[:, :, j0 : j0 + PACK], spread[:].rearrange("p j n -> p n j"), ACT.Copy)
-
+        by_token = keep.tile([P, 2 * PARTS], F32, name="by_token", tag="gate_then_bytes", align_bytes=64)
         gate2_by_token = keep.tile([P, PARTS], F32, name="gate2_by_token")
-        upright = psum.tile([P, PARTS, P], F32, name="upright", tag="small", bufs=2)
-        for q in range(PARTS):
-            nc.tensor.transpose(upright[:, q, :], gates[:, 1, q * P : (q + 1) * P], ident[:])
-        nc.scalar.activation(gate2_by_token[:], upright[:, :, 0], ACT.Copy)
+        upright = psum.tile([P, P], F32, name="upright", tag="small", bufs=2)
+        nc.tensor.transpose(upright[:], gate_rows[:], ident[:])
+        nc.scalar.activation(by_token[:], upright[:, : 2 * PARTS], ACT.Copy)
+        nc.scalar.activation(gate2_by_token[:], upright[:, PARTS : 2 * PARTS], ACT.Copy)
+
+        gates = keep.tile([P, 2, T], F32, name="gates", align_bytes=64)
+        for r in range(2):
+            spread = psum.tile([P, PARTS, P], F32, name="spread", tag="pair" if r else "single", bufs=2 if r else 1)
+            for q in range(PARTS):
+                column = by_token[:, r * PARTS + q : r * PARTS + q + 1]
+                nc.tensor.transpose(spread[:, q, :], column.to_broadcast([P, P]), ident[:])
+            nc.scalar.activation(gates[:, r, :], spread[:].rearrange("p q n -> p (q n)"), ACT.Copy)
 
         w2 = {}
 
@@ -155,7 +154,7 @@ def tile_moe_cpy_mlp_relu2_kernel(
                 nc.sync.dma_start(pos1_sb[:], pos1)
                 nc.sync.dma_start(pos2_sb[:], pos2)
                 load_w2(2)
-            nc.scalar.activation(wins[b][:, SLOTS + T :], zeros[:], ACT.Copy)
+            nc.scalar.activation(wins[b][:, SLOTS + T :], upright[:, P - PAD :], ACT.Copy)
 
         with tc.tile_pool(name="gathered", bufs=1, side="right") as gathered:
             words, scale_bytes = {}, {}
@@ -276,7 +275,7 @@ def tile_moe_cpy_mlp_relu2_kernel(
                 y = psum.tile([P, (e1 - e0) * C], F32, name="y", tag=tag, bufs=3 if tag == "sums" else 2)
                 for e in range(e0, e1):
                     expert_product(y[:, (e - e0) * C : (e - e0 + 1) * C], b, e)
-                if b == 0 and e0 >= WIDE_EXPERTS:
+                if b == 0:
                     nc.vector.tensor_copy(wins[b][:, e0 * C : e1 * C], y[:])
                 else:
                     nc.scalar.activation(wins[b][:, e0 * C : e1 * C], y[:], ACT.Copy)
@@ -284,8 +283,11 @@ def tile_moe_cpy_mlp_relu2_kernel(
         for b in range(BLOCKS):
             second_layer(b)
 
+        shared = list(range(SHARED_FROM, SHARED_TO))
+
         def gated(b, r, positions):
-            term = prods.tile([P, T], F32, name="term")
+            after = b + r - LAG - 1
+            term = prods.tile([P, T], F32, name="term", tag=f"scaled{after}" if after in shared else f"term{b}_{r}")
             nc.vector.tensor_tensor(term[:], wins[b][:].indirect(positions[:]), gates[:, r, :], ALU.mult)
             return term
 
@@ -305,8 +307,8 @@ def tile_moe_cpy_mlp_relu2_kernel(
 
         returned = []
 
-        def scale_and_return(there, cuts):
-            scaled = ring.tile([P, PARTS, P], F32, name="scaled", bufs=2)
+        def scale_and_return(b, there, cuts):
+            scaled = prods.tile([P, PARTS, P], F32, name="scaled", tag=f"scaled{b}")
             pieces = []
             for q0, q1 in cuts:
                 spare = len(returned) % BACK_BANKS == BACK_BANKS - 1
@@ -318,12 +320,11 @@ def tile_moe_cpy_mlp_relu2_kernel(
                 pieces.append((q0 * P, q1 * P, back[:].rearrange("p q t -> p (q t)")))
             return pieces
 
-        shared = list(range(SHARED_FROM, SHARED_TO))
         backs = {}
         there = fetch_and_turn(shared[0])
         for b in shared:
             ahead = fetch_and_turn(b + 1) if b + 1 in shared else None
-            backs[b] = scale_and_return(there, [(0, PARTS)] if ahead is not None else LAST_CUTS)
+            backs[b] = scale_and_return(b, there, [(0, PARTS)] if ahead is not None else LAST_CUTS)
             there = ahead
 
         firsts = {}

@@ -35,6 +35,7 @@ QUANTIZE_EXPERTS = [(0, 2), (2, 3), (3, 4), (4, 5), (5, 6)]
 EARLY_BLOCKS = 4
 EARLY_AFTER_TURN = 3
 W2_LOADS = [(0, 2, 0, 4), (2, 6, 0, 4), (0, 6, 4, 8)]
+VECTOR_COPIES = 2
 WIDE_EXPERTS = 4
 SHARED_FROM, SHARED_TO = 1, 7
 LAG = 4
@@ -275,7 +276,7 @@ def tile_moe_cpy_mlp_relu2_kernel(
                 y = psum.tile([P, (e1 - e0) * C], F32, name="y", tag=tag, bufs=3 if tag == "sums" else 2)
                 for e in range(e0, e1):
                     expert_product(y[:, (e - e0) * C : (e - e0 + 1) * C], b, e)
-                if b == 0:
+                if b < VECTOR_COPIES:
                     nc.vector.tensor_copy(wins[b][:, e0 * C : e1 * C], y[:])
                 else:
                     nc.scalar.activation(wins[b][:, e0 * C : e1 * C], y[:], ACT.Copy)
@@ -287,7 +288,7 @@ def tile_moe_cpy_mlp_relu2_kernel(
 
         def gated(b, r, positions):
             after = b + r - LAG - 1
-            term = prods.tile([P, T], F32, name="term", tag=f"scaled{after}" if after in shared else f"term{b}_{r}")
+            term = prods.tile([P, T], F32, name="term", tag=f"scaled{after}_0" if after in shared else f"term{b}_{r}")
             nc.vector.tensor_tensor(term[:], wins[b][:].indirect(positions[:]), gates[:, r, :], ALU.mult)
             return term
 
@@ -297,35 +298,39 @@ def tile_moe_cpy_mlp_relu2_kernel(
                 nc.vector.tensor_tensor(res[:], second, first[:, t0:t1], ALU.add)
                 nc.sync.dma_start(out[b * P : (b + 1) * P, t0:t1], res[:])
 
-        def fetch_and_turn(b):
-            raw = ring.tile([P, T], F32, name="raw", bufs=2)
-            nc.scalar.activation(raw[:], wins[b][:].indirect(pos2_sb[:]), ACT.Copy)
-            there = psum.tile([P, PARTS, P], F32, name="there", tag="pair", bufs=2)
-            for q in range(PARTS):
-                nc.tensor.transpose(there[:, q, :], raw[:, q * P : (q + 1) * P], ident[:])
-            return there
+        def fetch_and_turn(b, q0, q1):
+            raw = ring.tile([P, (q1 - q0) * P], F32, name="raw", bufs=2)
+            nc.scalar.activation(raw[:], wins[b][:].indirect(pos2_sb[:, q0 * P // 16 : q1 * P // 16]), ACT.Copy)
+            there = psum.tile([P, q1 - q0, P], F32, name="there", tag="pair", bufs=2)
+            for q in range(q0, q1):
+                nc.tensor.transpose(there[:, q - q0, :], raw[:, (q - q0) * P : (q - q0 + 1) * P], ident[:])
+            return there, q0
 
         returned = []
 
-        def scale_and_return(b, there, cuts):
-            scaled = prods.tile([P, PARTS, P], F32, name="scaled", tag=f"scaled{b}")
+        def scale_and_return(b, turned, cuts):
+            there, first_part = turned
+            scaled = prods.tile([P, PARTS, P], F32, name="scaled", tag=f"scaled{b}_{first_part}")
             pieces = []
             for q0, q1 in cuts:
                 spare = len(returned) % BACK_BANKS == BACK_BANKS - 1
                 back = psum.tile([P, q1 - q0, P], F32, name="back", tag="single" if spare else "sums", bufs=1 if spare else 3)
                 returned.append(back)
                 for q in range(q0, q1):
-                    nc.scalar.activation(scaled[:, q, :], there[:, q, :], ACT.Copy, scale=gate2_by_token[:, q : q + 1])
+                    nc.scalar.activation(scaled[:, q, :], there[:, q - first_part, :], ACT.Copy, scale=gate2_by_token[:, q : q + 1])
                     nc.tensor.transpose(back[:, q - q0, :], scaled[:, q, :], ident[:])
                 pieces.append((q0 * P, q1 * P, back[:].rearrange("p q t -> p (q t)")))
             return pieces
 
         backs = {}
-        there = fetch_and_turn(shared[0])
-        for b in shared:
-            ahead = fetch_and_turn(b + 1) if b + 1 in shared else None
-            backs[b] = scale_and_return(b, there, [(0, PARTS)] if ahead is not None else LAST_CUTS)
+        last = shared[-1]
+        there = fetch_and_turn(shared[0], 0, PARTS)
+        for b in shared[:-1]:
+            ahead = fetch_and_turn(b + 1, 0, PARTS if b + 1 < last else PARTS // 2)
+            backs[b] = scale_and_return(b, there, [(0, PARTS)])
             there = ahead
+        ahead = fetch_and_turn(last, PARTS // 2, PARTS)
+        backs[last] = scale_and_return(last, there, LAST_CUTS[:1]) + scale_and_return(last, ahead, LAST_CUTS[1:])
 
         firsts = {}
         waiting = []

@@ -98,29 +98,31 @@ def tile_moe_cpy_mlp_relu2_kernel(
         load_scales(w1s_b, [w1_rows[r][:, first_planes:, :] for r in range(4)])
 
         with tc.tile_pool(name="setup", bufs=1) as setup:
-            blank = setup.tile([P, P], F32, name="blank")
-            nc.vector.memset(blank[:], 0.0)
+            blank = setup.tile([P, P], I32, name="blank")
+            nc.vector.memset(blank[:], 0)
             nc.gpsimd.affine_select(
                 out=ident[:],
-                in_=blank[:],
+                in_=blank[:].bitcast(F32),
                 compare_op=ALU.not_equal,
                 fill=1.0,
                 base=0,
                 pattern=[[-1, P]],
                 channel_multiplier=1,
             )
+            zero_words = blank[:].bitcast(U32).unsqueeze(1).to_broadcast([P, PACK, P])
+            for c0 in range(0, E * K // PACK, H):
+                nc.scalar.copy(plane_c[:, c0 : c0 + H].bitcast(U32).rearrange("p (a w) -> p a w", a=PACK), zero_words)
 
-        zero_words = keep.tile([P, H], I32, name="zero_words")
-        nc.vector.memset(zero_words[:], 0)
-        for c0 in range(0, E * K // PACK, H):
-            nc.scalar.copy(plane_c[:, c0 : c0 + H].bitcast(U32), zero_words[:].bitcast(U32))
         big = ctx.enter_context(tc.tile_pool(name="big", bufs=1))
 
-        by_token = keep.tile([P, 2 * PARTS], F32, name="by_token", tag="gate_then_bytes", align_bytes=64)
+        held = ctx.enter_context(tc.tile_pool(name="held", bufs=1))
+        later_slots = (E - FIRST_EXPERTS) * C
+        room = held.tile([P, PASSES * later_slots * (PACK + 1) // PACK], F32, name="room", align_bytes=64, offset=0)
+        by_token = room[:, : 2 * PARTS]
         gate2_by_token = keep.tile([P, PARTS], F32, name="gate2_by_token")
         upright = psum.tile([P, P], F32, name="upright", tag="small", bufs=2)
         nc.tensor.transpose(upright[:], gate_rows[:], ident[:])
-        nc.scalar.activation(by_token[:], upright[:, : 2 * PARTS], ACT.Copy)
+        nc.scalar.activation(by_token, upright[:, : 2 * PARTS], ACT.Copy)
         nc.scalar.activation(gate2_by_token[:], upright[:, PARTS : 2 * PARTS], ACT.Copy)
 
         gates = keep.tile([P, 2, T], F32, name="gates", align_bytes=64)
@@ -160,7 +162,7 @@ def tile_moe_cpy_mlp_relu2_kernel(
         with tc.tile_pool(name="gathered", bufs=1, side="right") as gathered:
             words, scale_bytes = {}, {}
             first_bytes = gathered.tile([P, PASSES, FIRST_EXPERTS * C], U8, name="first_bytes", align_bytes=64)
-            later_bytes = keep.tile([P, PASSES, (E - FIRST_EXPERTS) * C], U8, name="later_bytes", tag="gate_then_bytes", align_bytes=64)
+            later_bytes = held.tile([P, PASSES, later_slots], U8, name="later_bytes", align_bytes=64, offset=0)
 
             def gather(e0, e1, s, into, window, found):
                 nc.vector.tensor_copy(into, window.indirect(offs_sb[:, e0 * C // 16 : e1 * C // 16]))
@@ -173,9 +175,12 @@ def tile_moe_cpy_mlp_relu2_kernel(
                     gather(e0, e1, s, into, xs[:, s, :].bitcast(U8), scale_bytes)
 
             def gather_words(e0, e1, s):
-                tile = gathered.tile([P, (e1 - e0) * C], U32, name=f"xg{s}_{e0}", align_bytes=64)
-                window = xw[:, s * T : T if (e0, s) == (0, 0) else PASSES * T]
-                gather(e0, e1, s, tile[:], window.bitcast(U32), words)
+                if e0 == 0:
+                    tile = gathered.tile([P, (e1 - e0) * C], U32, name=f"xg{s}_{e0}", align_bytes=64)
+                else:
+                    at = PASSES * later_slots + PACK * (s * later_slots + (e0 - FIRST_EXPERTS) * C)
+                    tile = held.tile([P, (e1 - e0) * C], U32, name=f"xg{s}_{e0}", align_bytes=64, offset=at)
+                gather(e0, e1, s, tile[:], xw[:, s * T : (s + 1) * T].bitcast(U32), words)
 
             gather_words(0, FIRST_EXPERTS, 0)
             for e0, e1 in BYTE_PIECES:
@@ -286,16 +291,15 @@ def tile_moe_cpy_mlp_relu2_kernel(
 
         shared = list(range(SHARED_FROM, SHARED_TO))
 
-        def gated(b, r, positions):
-            after = b + r - LAG - 1
-            term = prods.tile([P, T], F32, name="term", tag=f"scaled{after}_0" if after in shared else f"term{b}_{r}")
-            nc.vector.tensor_tensor(term[:], wins[b][:].indirect(positions[:]), gates[:, r, :], ALU.mult)
+        def gated(b, r, positions, after, t0=0, t1=T):
+            term = prods.tile([P, t1 - t0], F32, name="term", tag=f"scaled{after}_0" if after in shared else f"term{b}_{r}")
+            nc.vector.tensor_tensor(term[:], wins[b][:].indirect(positions[:, t0 // 16 : t1 // 16]), gates[:, r, t0:t1], ALU.mult)
             return term
 
-        def add_and_store(b, first, seconds):
+        def add_and_store(b, first, seconds, base=0):
             for t0, t1, second in seconds:
                 res = ring.tile([P, t1 - t0], F32, name="res", bufs=BLOCKS + len(LAST_CUTS) - 1)
-                nc.vector.tensor_tensor(res[:], second, first[:, t0:t1], ALU.add)
+                nc.vector.tensor_tensor(res[:], second, first[:, t0 - base : t1 - base], ALU.add)
                 nc.sync.dma_start(out[b * P : (b + 1) * P, t0:t1], res[:])
 
         def fetch_and_turn(b, q0, q1):
@@ -332,18 +336,21 @@ def tile_moe_cpy_mlp_relu2_kernel(
         ahead = fetch_and_turn(last, PARTS // 2, PARTS)
         backs[last] = scale_and_return(last, there, LAST_CUTS[:1]) + scale_and_return(last, ahead, LAST_CUTS[1:])
 
-        firsts = {}
-        waiting = []
-        for b in range(BLOCKS):
-            firsts[b] = gated(b, 0, pos1_sb)
-            if waiting:
-                add_and_store(*waiting.pop(0))
-            if b - LAG in shared:
-                add_and_store(b - LAG, firsts[b - LAG], backs[b - LAG])
-            if b not in shared:
-                waiting.append((b, firsts[b], [(0, T, gated(b, 1, pos2_sb)[:])]))
-        left = [b for b in shared if b + LAG >= BLOCKS]
-        add_and_store(left[0], firsts[left[0]], backs[left[0]])
-        add_and_store(*waiting.pop(0))
-        for b in left[1:]:
-            add_and_store(b, firsts[b], backs[b])
+        alone = BLOCKS - 1
+        firsts = {0: gated(0, 0, pos1_sb, None)}
+        second = gated(0, 1, pos2_sb, None)
+        firsts[1] = gated(1, 0, pos1_sb, None)
+        add_and_store(0, firsts[0], [(0, T, second[:])])
+        for b in list(range(2, LAG + 1)) + [alone]:
+            firsts[b] = gated(b, 0, pos1_sb, None)
+        add_and_store(1, firsts[1], backs[1])
+        second = gated(alone, 1, pos2_sb, 1)
+        add_and_store(2, firsts[2], backs[2])
+        add_and_store(alone, firsts[alone], [(0, T, second[:])])
+        for b in range(LAG + 1, alone):
+            firsts[b] = gated(b, 0, pos1_sb, b - LAG + 1, 0, T if b < last else T // 2)
+            add_and_store(b - LAG + 2, firsts[b - LAG + 2], backs[b - LAG + 2])
+        add_and_store(last - 1, firsts[last - 1], backs[last - 1])
+        other_half = gated(last, 0, pos1_sb, last - 1, T // 2, T)
+        add_and_store(last, firsts[last], backs[last][:1])
+        add_and_store(last, other_half, backs[last][1:], T // 2)

@@ -118,18 +118,18 @@ def tile_moe_cpy_mlp_relu2_kernel(
         held = ctx.enter_context(tc.tile_pool(name="held", bufs=1))
         later_slots = (E - FIRST_EXPERTS) * C
         room = held.tile([P, PASSES * later_slots * (PACK + 1) // PACK], F32, name="room", align_bytes=64, offset=0)
-        by_token = room[:, : 2 * PARTS]
+        gate1_by_token = room[:, :PARTS]
         gate2_by_token = keep.tile([P, PARTS], F32, name="gate2_by_token")
         upright = psum.tile([P, P], F32, name="upright", tag="small", bufs=2)
         nc.tensor.transpose(upright[:], gate_rows[:], ident[:])
-        nc.scalar.activation(by_token, upright[:, : 2 * PARTS], ACT.Copy)
+        nc.scalar.activation(gate1_by_token, upright[:, :PARTS], ACT.Copy)
         nc.scalar.activation(gate2_by_token[:], upright[:, PARTS : 2 * PARTS], ACT.Copy)
 
         gates = keep.tile([P, 2, T], F32, name="gates", align_bytes=64)
-        for r in range(2):
+        for r, by_token in enumerate((gate1_by_token, gate2_by_token[:])):
             spread = psum.tile([P, PARTS, P], F32, name="spread", tag="pair" if r else "single", bufs=2 if r else 1)
             for q in range(PARTS):
-                column = by_token[:, r * PARTS + q : r * PARTS + q + 1]
+                column = by_token[:, q : q + 1]
                 nc.tensor.transpose(spread[:, q, :], column.to_broadcast([P, P]), ident[:])
             nc.scalar.activation(gates[:, r, :], spread[:].rearrange("p q n -> p (q n)"), ACT.Copy)
 

@@ -21,11 +21,12 @@ PACK = 4
 PASSES = K // (P * PACK)
 SLOTS = E * C
 BLOCKS = K // P
+HALF = BLOCKS // 2
 PARTS = T // P
 WINDOW = SLOTS + T + PAD
 
 FIRST_EXPERTS = 2
-W1_LOADS = [(0, 1), (1, 2), (2, 4), (4, 6)]
+W1_LOADS = [(0, 1), (1, 2), (2, 4), (4, 5), (5, 6)]
 BYTE_PIECES = [(0, 2), (2, 4), (4, 6)]
 WORD_PIECES = [(0, 2), (2, 4), (4, 5), (5, 6)]
 VECTOR_RELU_FROM = 4
@@ -60,7 +61,7 @@ def tile_moe_cpy_mlp_relu2_kernel(
         xs = keep.tile([P, PASSES, T // PACK], I32, name="xs", align_bytes=64)
         plane_a = keep.tile([P, FIRST_EXPERTS * K // PACK], I32, name="plane_a", align_bytes=64)
         plane_b = keep.tile([P, (E - FIRST_EXPERTS) * K // PACK], I32, name="plane_b", align_bytes=64)
-        plane_c = keep.tile([P, E * K // PACK], I32, name="plane_c", align_bytes=64)
+        planes_c = [keep.tile([P, E, HALF * P // PACK], I32, name=f"plane_c{h}", align_bytes=64) for h in range(2)]
         ident = keep.tile([P, P], F32, name="ident")
         hb = keep.tile([P, SLOTS, PACK], BF16, name="hb", align_bytes=64)
         hq = keep.tile([P, SLOTS], U32, name="hq", align_bytes=64)
@@ -109,9 +110,10 @@ def tile_moe_cpy_mlp_relu2_kernel(
                 pattern=[[-1, P]],
                 channel_multiplier=1,
             )
-            zero_words = blank[:].bitcast(U32).unsqueeze(1).to_broadcast([P, PACK, P])
-            for c0 in range(0, E * K // PACK, H):
-                nc.scalar.copy(plane_c[:, c0 : c0 + H].bitcast(U32).rearrange("p (a w) -> p a w", a=PACK), zero_words)
+            zero_words = blank[:].bitcast(U32).unsqueeze(1).to_broadcast([P, E // 2, P])
+            for plane in planes_c:
+                for e0 in range(0, E, E // 2):
+                    nc.scalar.copy(plane[:, e0 : e0 + E // 2, :].bitcast(U32), zero_words)
 
         big = ctx.enter_context(tc.tile_pool(name="big", bufs=1))
 
@@ -146,8 +148,8 @@ def tile_moe_cpy_mlp_relu2_kernel(
 
         for n in range(FIRST_EXPERTS, len(W1_LOADS)):
             load_w1(big, n)
-        w2_planes = plane_c[:].rearrange("p (e n) -> p e n", e=E)
-        load_scales(w2_planes, w2_scales.rearrange("e o (q r) n -> r q (e o) n", r=4))
+        w2_rows = w2_scales.rearrange("e o (q r) n -> r q (e o) n", r=4)
+        load_scales(planes_c[0], [w2_rows[r][:, :, : HALF * P] for r in range(4)])
         wins = [big.tile([P, WINDOW], F32, name=f"win{b}") for b in range(BLOCKS)]
         load_w2(0)
         load_w2(1)
@@ -156,6 +158,7 @@ def tile_moe_cpy_mlp_relu2_kernel(
             if b == 0:
                 nc.sync.dma_start(pos1_sb[:], pos1)
                 nc.sync.dma_start(pos2_sb[:], pos2)
+                load_scales(planes_c[1], [w2_rows[r][:, :, HALF * P :] for r in range(4)])
                 load_w2(2)
             nc.scalar.activation(wins[b][:, SLOTS + T :], upright[:, P - PAD :], ACT.Copy)
 
@@ -195,7 +198,7 @@ def tile_moe_cpy_mlp_relu2_kernel(
                 nc.tensor.matmul_mx(
                     out=into,
                     lhsT=w2[b, e].bitcast(FP4X4),
-                    lhsT_scale=w2_planes[:, e, b * P // PACK : (b + 1) * P // PACK].bitcast(U8),
+                    lhsT_scale=planes_c[b // HALF][:, e, b % HALF * P // PACK : (b % HALF + 1) * P // PACK].bitcast(U8),
                     rhs=hq[:, cols].bitcast(FP8X4),
                     rhs_scale=hs[:, cols],
                     start=True,

@@ -35,7 +35,7 @@ TURNS_AFTER = {1: (0, 1), 5: (2, 3, 5, 4)}
 QUANTIZE_EXPERTS = [(0, 2), (2, 3), (3, 4), (4, 5), (5, 6)]
 EARLY_BLOCKS = 4
 EARLY_AFTER_TURN = 3
-W2_LOADS = [(0, 2, 0, 4), (2, 6, 0, 4), (0, 6, 4, 8)]
+W2_LOADS = [(0, 2, 0, 4), (2, 6, 0, 4), (0, 6, 4, 6), (0, 6, 6, 8)]
 VECTOR_COPIES = 2
 WIDE_EXPERTS = 4
 SHARED_FROM, SHARED_TO = 1, 7
@@ -160,6 +160,8 @@ def tile_moe_cpy_mlp_relu2_kernel(
                 nc.sync.dma_start(pos2_sb[:], pos2)
                 load_scales(planes_c[1], [w2_rows[r][:, :, HALF * P :] for r in range(4)])
                 load_w2(2)
+            if b == 1:
+                load_w2(3)
             nc.scalar.activation(wins[b][:, SLOTS + T :], upright[:, P - PAD :], ACT.Copy)
 
         with tc.tile_pool(name="gathered", bufs=1, side="right") as gathered:

@@ -36,7 +36,6 @@ QUANTIZE_EXPERTS = [(0, 2), (2, 3), (3, 4), (4, 5), (5, 6)]
 EARLY_BLOCKS = 4
 EARLY_AFTER_TURN = 3
 W2_LOADS = [(0, 2, 0, 4), (2, 6, 0, 4), (0, 6, 4, 6), (0, 6, 6, 8)]
-VECTOR_COPIES = 2
 WIDE_EXPERTS = 4
 SHARED_FROM, SHARED_TO = 1, 7
 LAG = 4
@@ -278,6 +277,8 @@ def tile_moe_cpy_mlp_relu2_kernel(
             if b < EARLY_BLOCKS:
                 nc.scalar.activation(wins[b][:, : FIRST_EXPERTS * C], early[b], ACT.Copy)
                 groups = [("pair", FIRST_EXPERTS, E)]
+            if b == 1:
+                groups = [("pair", FIRST_EXPERTS, WIDE_EXPERTS), ("small", WIDE_EXPERTS, E)]
             if b == 0:
                 groups = [("pair", FIRST_EXPERTS, WIDE_EXPERTS)] + [("small", e, e + 1) for e in range(WIDE_EXPERTS, E)]
             for tag, e0, e1 in groups:
@@ -286,7 +287,7 @@ def tile_moe_cpy_mlp_relu2_kernel(
                 y = psum.tile([P, (e1 - e0) * C], F32, name="y", tag=tag, bufs=3 if tag == "sums" else 2)
                 for e in range(e0, e1):
                     expert_product(y[:, (e - e0) * C : (e - e0 + 1) * C], b, e)
-                if b < VECTOR_COPIES:
+                if b == 0 or (b, e0) == (1, FIRST_EXPERTS):
                     nc.vector.tensor_copy(wins[b][:, e0 * C : e1 * C], y[:])
                 else:
                     nc.scalar.activation(wins[b][:, e0 * C : e1 * C], y[:], ACT.Copy)

@@ -36,6 +36,7 @@ QUANTIZE_EXPERTS = [(0, 2), (2, 3), (3, 4), (4, 5), (5, 6)]
 EARLY_BLOCKS = 4
 EARLY_AFTER_TURN = 3
 W2_LOADS = [(0, 2, 0, 4), (2, 6, 0, 4), (0, 6, 4, 6), (0, 6, 6, 8)]
+HALVED = (1,)
 WIDE_EXPERTS = 4
 SHARED_FROM, SHARED_TO = 1, 7
 LAG = 4
@@ -244,28 +245,32 @@ def tile_moe_cpy_mlp_relu2_kernel(
 
             relus = []
             for e in range(E):
-                pre = psum.tile([P, H], F32, name="pre", tag="sums")
-                for s in range(PASSES):
-                    plane = w1s_a[:, e * PASSES + s, :] if e < FIRST_EXPERTS else w1s_b[:, e * PASSES + s - first_planes, :]
-                    nc.tensor.matmul_mx(
-                        out=pre[:],
-                        lhsT=words[e, s].bitcast(FP8X4),
-                        lhsT_scale=scale_bytes[e, s],
-                        rhs=w1[e][:, s, :].bitcast(FP4X4),
-                        rhs_scale=plane.bitcast(U8),
-                        start=(s == 0),
-                        stop=(s == PASSES - 1),
-                    )
                 relu = ring.tile([P, PACK, P], F32, name="relu", bufs=E)
-                by_place = relu[:]
-                sums = pre[:].rearrange("p (m d) -> p d m", d=PACK)
-                if e == WORD_TURNED:
-                    by_place = relu[:].rearrange("p d m -> p (d m)").rearrange("p (u m c) -> p u m c", u=2, c=2)
-                    sums = pre[:].rearrange("p (m u c) -> p u m c", u=2, c=2)
-                if e < VECTOR_RELU_FROM:
-                    nc.scalar.activation(by_place, sums, ACT.Relu)
-                else:
-                    nc.vector.tensor_scalar_max(by_place, sums, 0.0)
+                cuts = 2 if e in HALVED else 1
+                width = H // cuts
+                for cut in range(cuts):
+                    spare = e == HALVED[0] and cut == 0
+                    pre = psum.tile([P, width], F32, name="pre", tag="small" if spare else "sums", bufs=2 if spare else 3)
+                    for s in range(PASSES):
+                        plane = w1s_a[:, e * PASSES + s, :] if e < FIRST_EXPERTS else w1s_b[:, e * PASSES + s - first_planes, :]
+                        nc.tensor.matmul_mx(
+                            out=pre[:],
+                            lhsT=words[e, s].bitcast(FP8X4),
+                            lhsT_scale=scale_bytes[e, s],
+                            rhs=w1[e][:, s, 2 * cut * width : 2 * (cut + 1) * width].bitcast(FP4X4),
+                            rhs_scale=plane.bitcast(U8)[:, cut * width : (cut + 1) * width],
+                            start=(s == 0),
+                            stop=(s == PASSES - 1),
+                        )
+                    by_place = relu[:, :, cut * width // PACK : (cut + 1) * width // PACK]
+                    sums = pre[:].rearrange("p (m d) -> p d m", d=PACK)
+                    if e == WORD_TURNED:
+                        by_place = relu[:].rearrange("p d m -> p (d m)").rearrange("p (u m c) -> p u m c", u=2, c=2)
+                        sums = pre[:].rearrange("p (m u c) -> p u m c", u=2, c=2)
+                    if e < VECTOR_RELU_FROM:
+                        nc.scalar.activation(by_place, sums, ACT.Relu)
+                    else:
+                        nc.vector.tensor_scalar_max(by_place, sums, 0.0)
                 relus.append(relu)
                 for due in TURNS_AFTER.get(e, ()):
                     turn_and_square(due, relus[due])

@@ -36,7 +36,7 @@ QUANTIZE_EXPERTS = [(0, 2), (2, 3), (3, 4), (4, 5), (5, 6)]
 EARLY_BLOCKS = 4
 EARLY_AFTER_TURN = 3
 W2_LOADS = [(0, 2, 0, 4), (2, 6, 0, 4), (0, 6, 4, 6), (0, 6, 6, 8)]
-HALVED = (1,)
+HALVED = (1, 5)
 WIDE_EXPERTS = 4
 SHARED_FROM, SHARED_TO = 1, 7
 LAG = 4
@@ -249,7 +249,7 @@ def tile_moe_cpy_mlp_relu2_kernel(
                 cuts = 2 if e in HALVED else 1
                 width = H // cuts
                 for cut in range(cuts):
-                    spare = e == HALVED[0] and cut == 0
+                    spare = e in HALVED and cut == 0
                     pre = psum.tile([P, width], F32, name="pre", tag="small" if spare else "sums", bufs=2 if spare else 3)
                     for s in range(PASSES):
                         plane = w1s_a[:, e * PASSES + s, :] if e < FIRST_EXPERTS else w1s_b[:, e * PASSES + s - first_planes, :]

@@ -85,19 +85,7 @@ def tile_moe_cpy_mlp_relu2_kernel(
         first_planes = FIRST_EXPERTS * PASSES
         nc.vector.memset(xs[:], 0)
         gate_rows = keep.tile([P, P], F32, name="gate_rows")
-        nc.gpsimd.memset(gate_rows[:], 0.0)
-        nc.gpsimd.memset(plane_a[:], 0)
-        nc.vector.memset(plane_b[:], 0)
-        nc.sync.dma_start(offs_sb[:], offs)
-        nc.sync.dma_start(xw[:, :T], x_words[0].rearrange("p t d -> p (t d)").bitcast(I32))
-        nc.sync.dma_start(gate_rows[: 2 * PARTS, :], gate[:, 0, :].rearrange("r (q n) -> r q n", n=P))
-        load_scales(xs, x_scales.rearrange("s (q r) t -> r q s t", r=4))
-        nc.sync.dma_start(xw[:, T:], x_words[1].rearrange("p t d -> p (t d)").bitcast(I32))
-        load_w1(keep, 0)
-        load_scales(w1s_a, [w1_rows[r][:, :first_planes, :] for r in range(4)])
-        load_w1(keep, 1)
-        load_scales(w1s_b, [w1_rows[r][:, first_planes:, :] for r in range(4)])
-
+        nc.vector.memset(gate_rows[:], 0.0)
         with tc.tile_pool(name="setup", bufs=1) as setup:
             blank = setup.tile([P, P], I32, name="blank")
             nc.vector.memset(blank[:], 0)
@@ -114,6 +102,18 @@ def tile_moe_cpy_mlp_relu2_kernel(
             for plane in planes_c:
                 for e0 in range(0, E, E // 2):
                     nc.scalar.copy(plane[:, e0 : e0 + E // 2, :].bitcast(U32), zero_words)
+
+        nc.vector.memset(plane_a[:], 0)
+        nc.vector.memset(plane_b[:], 0)
+        nc.sync.dma_start(offs_sb[:], offs)
+        nc.sync.dma_start(xw[:, :T], x_words[0].rearrange("p t d -> p (t d)").bitcast(I32))
+        nc.sync.dma_start(gate_rows[: 2 * PARTS, :], gate[:, 0, :].rearrange("r (q n) -> r q n", n=P))
+        load_scales(xs, x_scales.rearrange("s (q r) t -> r q s t", r=4))
+        nc.sync.dma_start(xw[:, T:], x_words[1].rearrange("p t d -> p (t d)").bitcast(I32))
+        load_w1(keep, 0)
+        load_scales(w1s_a, [w1_rows[r][:, :first_planes, :] for r in range(4)])
+        load_w1(keep, 1)
+        load_scales(w1s_b, [w1_rows[r][:, first_planes:, :] for r in range(4)])
 
         big = ctx.enter_context(tc.tile_pool(name="big", bufs=1))
 

@@ -107,8 +107,8 @@ def tile_moe_cpy_mlp_relu2_kernel(
         nc.vector.memset(plane_b[:], 0)
         nc.sync.dma_start(offs_sb[:], offs)
         nc.sync.dma_start(xw[:, :T], x_words[0].rearrange("p t d -> p (t d)").bitcast(I32))
-        nc.sync.dma_start(gate_rows[: 2 * PARTS, :], gate[:, 0, :].rearrange("r (q n) -> r q n", n=P))
         load_scales(xs, x_scales.rearrange("s (q r) t -> r q s t", r=4))
+        nc.sync.dma_start(gate_rows[: 2 * PARTS, :], gate[:, 0, :].rearrange("r (q n) -> r q n", n=P))
         nc.sync.dma_start(xw[:, T:], x_words[1].rearrange("p t d -> p (t d)").bitcast(I32))
         load_w1(keep, 0)
         load_scales(w1s_a, [w1_rows[r][:, :first_planes, :] for r in range(4)])

from contextlib import ExitStack

import concourse.mybir as mybir

K, T, E, C, H, PAD = 1024, 512, 6, 128, 512, 64
FLOPS = 2 * 2 * E * C * K * H

F32 = mybir.dt.float32
BF16 = mybir.dt.bfloat16
I32 = mybir.dt.int32
U32 = mybir.dt.uint32
U16 = mybir.dt.uint16
U8 = mybir.dt.uint8
FP8X4 = mybir.dt.float8_e4m3fn_x4
FP4X4 = mybir.dt.float4_e2m1fn_x4
ACT = mybir.ActivationFunctionType
ALU = mybir.AluOpType

P = 128
PACK = 4
PASSES = K // (P * PACK)
SLOTS = E * C
BLOCKS = K // P
HALF = BLOCKS // 2
PARTS = T // P
WINDOW = SLOTS + T + PAD

FIRST_EXPERTS = 2
W1_LOADS = [(0, 1), (1, 2), (2, 4), (4, 5), (5, 6)]
BYTE_PIECES = [(0, 2), (2, 4), (4, 6)]
WORD_PIECES = [(0, 2), (2, 4), (4, 5), (5, 6)]
VECTOR_RELU_FROM = 4
WORD_TURNED = 4
TURNS_AFTER = {1: (0, 1), 5: (2, 3, 5, 4)}
QUANTIZE_EXPERTS = [(0, 2), (2, 3), (3, 4), (4, 5), (5, 6)]
EARLY_BLOCKS = 4
EARLY_AFTER_TURN = 3
W2_LOADS = [(0, 2, 0, 4), (2, 6, 0, 4), (0, 6, 4, 6), (0, 6, 6, 8)]
HALVED = (1, 5)
WIDE_EXPERTS = 4
SHARED_FROM, SHARED_TO = 1, 7
LAG = 4
LAST_CUTS = [(0, 2), (2, 3), (3, 4)]
BACK_BANKS = 4


def tile_moe_cpy_mlp_relu2_kernel(
    tc, x_words, x_scales, xr, w1_words, w1_scales, w2_words, w2_scales, gate, offs, pos1, pos2, out
):
    nc = tc.nc
    with ExitStack() as ctx:
        keep = ctx.enter_context(tc.tile_pool(name="keep", bufs=1))
        ring = ctx.enter_context(tc.tile_pool(name="ring", bufs=3))
        prods = ctx.enter_context(tc.tile_pool(name="prods", bufs=1))
        psum = ctx.enter_context(tc.psum_pool(name="psum", bufs=3))

        offs_sb = keep.tile([P, SLOTS // 16], U16, name="offs_sb")
        pos1_sb = keep.tile([P, T // 16], U16, name="pos1_sb")
        pos2_sb = keep.tile([P, T // 16], U16, name="pos2_sb")
        xw = keep.tile([P, PASSES * T], I32, name="xw", align_bytes=64)
        xs = keep.tile([P, PASSES, T // PACK], I32, name="xs", align_bytes=64)
        plane_a = keep.tile([P, FIRST_EXPERTS * K // PACK], I32, name="plane_a", align_bytes=64)
        plane_b = keep.tile([P, (E - FIRST_EXPERTS) * K // PACK], I32, name="plane_b", align_bytes=64)
        planes_c = [keep.tile([P, E, HALF * P // PACK], I32, name=f"plane_c{h}", align_bytes=64) for h in range(2)]
        ident = keep.tile([P, P], F32, name="ident")
        hb = keep.tile([P, SLOTS, PACK], BF16, name="hb", align_bytes=64)
        hq = keep.tile([P, SLOTS], U32, name="hq", align_bytes=64)
        hs = keep.tile([P, SLOTS], U8, name="hs", align_bytes=64)

        def load_scales(plane, rows):
            for r in range(4):
                nc.sync.dma_start(plane[r:P:32], rows[r].bitcast(I32))

        w1 = []

        def load_w1(pool, n):
            e0, e1 = W1_LOADS[n]
            tile = pool.tile([P, (e1 - e0) * PASSES, 2 * H], U8, name=f"w1_{n}", tag=f"slot{n}", align_bytes=64)
            nc.sync.dma_start(tile[:].bitcast(I32), w1_words[e0:e1].rearrange("e s p c -> p (e s) c").bitcast(I32))
            w1.extend(tile[:, (e - e0) * PASSES : (e - e0 + 1) * PASSES, :] for e in range(e0, e1))

        w1s_a = plane_a[:].rearrange("p (g i) -> p g i", i=H // PACK)
        w1s_b = plane_b[:].rearrange("p (g i) -> p g i", i=H // PACK)
        w1_rows = w1_scales.rearrange("e s (q r) i -> r q (e s) i", r=4)
        first_planes = FIRST_EXPERTS * PASSES
        nc.vector.memset(xs[:], 0)
        gate_rows = keep.tile([P, P], F32, name="gate_rows")
        nc.vector.memset(gate_rows[:], 0.0)
        with tc.tile_pool(name="setup", bufs=1) as setup:
            blank = setup.tile([P, P], I32, name="blank")
            nc.vector.memset(blank[:], 0)
            nc.gpsimd.affine_select(
                out=ident[:],
                in_=blank[:].bitcast(F32),
                compare_op=ALU.not_equal,
                fill=1.0,
                base=0,
                pattern=[[-1, P]],
                channel_multiplier=1,
            )
            zero_words = blank[:].bitcast(U32).unsqueeze(1).to_broadcast([P, E // 2, P])
            for plane in planes_c:
                for e0 in range(0, E, E // 2):
                    nc.scalar.copy(plane[:, e0 : e0 + E // 2, :].bitcast(U32), zero_words)

        nc.vector.memset(plane_a[:], 0)
        nc.vector.memset(plane_b[:], 0)
        nc.sync.dma_start(offs_sb[:], offs)
        nc.sync.dma_start(xw[:, :T], x_words[0].rearrange("p t d -> p (t d)").bitcast(I32))
        load_scales(xs, x_scales.rearrange("s (q r) t -> r q s t", r=4))
        nc.sync.dma_start(gate_rows[: 2 * PARTS, :], gate[:, 0, :].rearrange("r (q n) -> r q n", n=P))
        nc.sync.dma_start(xw[:, T:], x_words[1].rearrange("p t d -> p (t d)").bitcast(I32))
        load_w1(keep, 0)
        load_scales(w1s_a, [w1_rows[r][:, :first_planes, :] for r in range(4)])
        load_w1(keep, 1)
        load_scales(w1s_b, [w1_rows[r][:, first_planes:, :] for r in range(4)])

        big = ctx.enter_context(tc.tile_pool(name="big", bufs=1))

        held = ctx.enter_context(tc.tile_pool(name="held", bufs=1))
        later_slots = (E - FIRST_EXPERTS) * C
        room = held.tile([P, PASSES * later_slots * (PACK + 1) // PACK], F32, name="room", align_bytes=64, offset=0)
        gate1_by_token = room[:, :PARTS]
        gate2_by_token = keep.tile([P, PARTS], F32, name="gate2_by_token")
        upright = psum.tile([P, P], F32, name="upright", tag="small", bufs=2)
        nc.tensor.transpose(upright[:], gate_rows[:], ident[:])
        nc.scalar.activation(gate1_by_token, upright[:, :PARTS], ACT.Copy)
        nc.scalar.activation(gate2_by_token[:], upright[:, PARTS : 2 * PARTS], ACT.Copy)

        gates = keep.tile([P, 2, T], F32, name="gates", align_bytes=64)
        for r, by_token in enumerate((gate1_by_token, gate2_by_token[:])):
            spread = psum.tile([P, PARTS, P], F32, name="spread", tag="pair" if r else "single", bufs=2 if r else 1)
            for q in range(PARTS):
                column = by_token[:, q : q + 1]
                nc.tensor.transpose(spread[:, q, :], column.to_broadcast([P, P]), ident[:])
            nc.scalar.activation(gates[:, r, :], spread[:].rearrange("p q n -> p (q n)"), ACT.Copy)

        w2 = {}

        def load_w2(n):
            e0, e1, b0, b1 = W2_LOADS[n]
            tile = big.tile([P, e1 - e0, (b1 - b0) * 2 * P], U8, name=f"w2_{n}", align_bytes=64)
            src = w2_words[e0:e1].rearrange("e o p c -> p (e o) c")[:, :, b0 * 2 * P : b1 * 2 * P]
            nc.sync.dma_start(tile[:].bitcast(I32), src.bitcast(I32))
            for e in range(e0, e1):
                for b in range(b0, b1):
                    w2[b, e] = tile[:, e - e0, (b - b0) * 2 * P : (b - b0 + 1) * 2 * P]

        for n in range(FIRST_EXPERTS, len(W1_LOADS)):
            load_w1(big, n)
        w2_rows = w2_scales.rearrange("e o (q r) n -> r q (e o) n", r=4)
        load_scales(planes_c[0], [w2_rows[r][:, :, : HALF * P] for r in range(4)])
        wins = [big.tile([P, WINDOW], F32, name=f"win{b}") for b in range(BLOCKS)]
        load_w2(0)
        load_w2(1)
        for b in range(BLOCKS):
            nc.sync.dma_start(wins[b][:, SLOTS : SLOTS + T], xr[b * P : (b + 1) * P, :])
            if b == 0:
                nc.sync.dma_start(pos1_sb[:], pos1)
                nc.sync.dma_start(pos2_sb[:], pos2)
                load_scales(planes_c[1], [w2_rows[r][:, :, HALF * P :] for r in range(4)])
                load_w2(2)
            if b == 1:
                load_w2(3)
            nc.scalar.activation(wins[b][:, SLOTS + T :], upright[:, P - PAD :], ACT.Copy)

        with tc.tile_pool(name="gathered", bufs=1, side="right") as gathered:
            words, scale_bytes = {}, {}
            first_bytes = gathered.tile([P, PASSES, FIRST_EXPERTS * C], U8, name="first_bytes", align_bytes=64)
            later_bytes = held.tile([P, PASSES, later_slots], U8, name="later_bytes", align_bytes=64, offset=0)

            def gather(e0, e1, s, into, window, found):
                nc.vector.tensor_copy(into, window.indirect(offs_sb[:, e0 * C // 16 : e1 * C // 16]))
                for e in range(e0, e1):
                    found[e, s] = into[:, (e - e0) * C : (e - e0 + 1) * C]

            def gather_bytes(e0, e1):
                for s in range(PASSES):
                    into = first_bytes[:, s, :] if e0 == 0 else later_bytes[:, s, (e0 - FIRST_EXPERTS) * C : (e1 - FIRST_EXPERTS) * C]
                    gather(e0, e1, s, into, xs[:, s, :].bitcast(U8), scale_bytes)

            def gather_words(e0, e1, s):
                if e0 == 0:
                    tile = gathered.tile([P, (e1 - e0) * C], U32, name=f"xg{s}_{e0}", align_bytes=64)
                else:
                    at = PASSES * later_slots + PACK * (s * later_slots + (e0 - FIRST_EXPERTS) * C)
                    tile = held.tile([P, (e1 - e0) * C], U32, name=f"xg{s}_{e0}", align_bytes=64, offset=at)
                gather(e0, e1, s, tile[:], xw[:, s * T : (s + 1) * T].bitcast(U32), words)

            gather_words(0, FIRST_EXPERTS, 0)
            for e0, e1 in BYTE_PIECES:
                gather_bytes(e0, e1)
                for first_expert, end_expert in WORD_PIECES:
                    if e0 <= first_expert < e1:
                        for s in range(1 if first_expert == 0 else 0, PASSES):
                            gather_words(first_expert, end_expert, s)

            def expert_product(into, b, e):
                cols = slice(e * C, (e + 1) * C)
                nc.tensor.matmul_mx(
                    out=into,
                    lhsT=w2[b, e].bitcast(FP4X4),
                    lhsT_scale=planes_c[b // HALF][:, e, b % HALF * P // PACK : (b % HALF + 1) * P // PACK].bitcast(U8),
                    rhs=hq[:, cols].bitcast(FP8X4),
                    rhs_scale=hs[:, cols],
                    start=True,
                    stop=True,
                )

            early = []

            def early_products():
                for b0 in range(0, EARLY_BLOCKS, 2):
                    y = psum.tile([P, 2, FIRST_EXPERTS * C], F32, name="early_y", tag="sums")
                    for j in range(2):
                        for e in range(FIRST_EXPERTS):
                            expert_product(y[:, j, e * C : (e + 1) * C], b0 + j, e)
                        early.append(y[:, j, :])

            squared = set()

            def turn_and_square(e, relu):
                cols = slice(e * C, (e + 1) * C)
                turned = psum.tile([P, PACK, C], F32, name="turned", tag="pair" if e % 3 else "single", bufs=2 if e % 3 else 1)
                if e == WORD_TURNED:
                    h = ring.tile([P, 2, 2 * P], BF16, name="h", bufs=1)
                    flat = relu[:].rearrange("p (u a) m -> p u (a m)", u=2)
                    nc.vector.tensor_tensor(h[:], flat, flat, ALU.mult)
                    for u in range(2):
                        nc.tensor.transpose(turned[:, u, :], h[:, u, :].bitcast(F32), ident[:])
                    nc.vector.tensor_copy(hb[:, cols, :].bitcast(F32), turned[:, :2, :].rearrange("p u s -> p s u"))
                else:
                    for d in range(PACK):
                        nc.tensor.transpose(turned[:, d, :], relu[:, d, :], ident[:])
                    nc.scalar.activation(hb[:, cols, :], turned[:].rearrange("p d s -> p s d"), ACT.Square)
                squared.add(e)
                for e0, e1 in QUANTIZE_EXPERTS:
                    if e0 <= e < e1 and all(other in squared for other in range(e0, e1)):
                        ready = slice(e0 * C, e1 * C)
                        nc.vector.quantize_mx(
                            out=hq[:, ready].bitcast(FP8X4),
                            scales=hs[:, ready],
                            in_=hb[:, ready, :].rearrange("p u j -> p (u j)"),
                        )

            relus = []
            for e in range(E):
                relu = ring.tile([P, PACK, P], F32, name="relu", bufs=E)
                cuts = 2 if e in HALVED else 1
                width = H // cuts
                for cut in range(cuts):
                    spare = e in HALVED and cut == 0
                    pre = psum.tile([P, width], F32, name="pre", tag="small" if spare else "sums", bufs=2 if spare else 3)
                    for s in range(PASSES):
                        plane = w1s_a[:, e * PASSES + s, :] if e < FIRST_EXPERTS else w1s_b[:, e * PASSES + s - first_planes, :]
                        nc.tensor.matmul_mx(
                            out=pre[:],
                            lhsT=words[e, s].bitcast(FP8X4),
                            lhsT_scale=scale_bytes[e, s],
                            rhs=w1[e][:, s, 2 * cut * width : 2 * (cut + 1) * width].bitcast(FP4X4),
                            rhs_scale=plane.bitcast(U8)[:, cut * width : (cut + 1) * width],
                            start=(s == 0),
                            stop=(s == PASSES - 1),
                        )
                    by_place = relu[:, :, cut * width // PACK : (cut + 1) * width // PACK]
                    sums = pre[:].rearrange("p (m d) -> p d m", d=PACK)
                    if e == WORD_TURNED:
                        by_place = relu[:].rearrange("p d m -> p (d m)").rearrange("p (u m c) -> p u m c", u=2, c=2)
                        sums = pre[:].rearrange("p (m u c) -> p u m c", u=2, c=2)
                    if e < VECTOR_RELU_FROM:
                        nc.scalar.activation(by_place, sums, ACT.Relu)
                    else:
                        nc.vector.tensor_scalar_max(by_place, sums, 0.0)
                relus.append(relu)
                for due in TURNS_AFTER.get(e, ()):
                    turn_and_square(due, relus[due])
                    if due == EARLY_AFTER_TURN:
                        early_products()

        def second_layer(b):
            groups = [("pair", 0, WIDE_EXPERTS), ("small", WIDE_EXPERTS, E)]
            if b < EARLY_BLOCKS:
                nc.scalar.activation(wins[b][:, : FIRST_EXPERTS * C], early[b], ACT.Copy)
                groups = [("pair", FIRST_EXPERTS, E)]
            if b == 1:
                groups = [("pair", FIRST_EXPERTS, WIDE_EXPERTS), ("small", WIDE_EXPERTS, E)]
            if b == 0:
                groups = [("pair", FIRST_EXPERTS, WIDE_EXPERTS)] + [("small", e, e + 1) for e in range(WIDE_EXPERTS, E)]
            for tag, e0, e1 in groups:
                if tag == "pair" and b % 2:
                    tag = "sums"
                y = psum.tile([P, (e1 - e0) * C], F32, name="y", tag=tag, bufs=3 if tag == "sums" else 2)
                for e in range(e0, e1):
                    expert_product(y[:, (e - e0) * C : (e - e0 + 1) * C], b, e)
                if b == 0 or (b, e0) == (1, FIRST_EXPERTS):
                    nc.vector.tensor_copy(wins[b][:, e0 * C : e1 * C], y[:])
                else:
                    nc.scalar.activation(wins[b][:, e0 * C : e1 * C], y[:], ACT.Copy)

        for b in range(BLOCKS):
            second_layer(b)

        shared = list(range(SHARED_FROM, SHARED_TO))

        def gated(b, r, positions, after, t0=0, t1=T):
            term = prods.tile([P, t1 - t0], F32, name="term", tag=f"scaled{after}_0" if after in shared else f"term{b}_{r}")
            nc.vector.tensor_tensor(term[:], wins[b][:].indirect(positions[:, t0 // 16 : t1 // 16]), gates[:, r, t0:t1], ALU.mult)
            return term

        def add_and_store(b, first, seconds, base=0):
            for t0, t1, second in seconds:
                res = ring.tile([P, t1 - t0], F32, name="res", bufs=BLOCKS + len(LAST_CUTS) - 1)
                nc.vector.tensor_tensor(res[:], second, first[:, t0 - base : t1 - base], ALU.add)
                nc.sync.dma_start(out[b * P : (b + 1) * P, t0:t1], res[:])

        def fetch_and_turn(b, q0, q1):
            raw = ring.tile([P, (q1 - q0) * P], F32, name="raw", bufs=2)
            nc.scalar.activation(raw[:], wins[b][:].indirect(pos2_sb[:, q0 * P // 16 : q1 * P // 16]), ACT.Copy)
            there = psum.tile([P, q1 - q0, P], F32, name="there", tag="pair", bufs=2)
            for q in range(q0, q1):
                nc.tensor.transpose(there[:, q - q0, :], raw[:, (q - q0) * P : (q - q0 + 1) * P], ident[:])
            return there, q0

        returned = []

        def scale_and_return(b, turned, cuts):
            there, first_part = turned
            scaled = prods.tile([P, PARTS, P], F32, name="scaled", tag=f"scaled{b}_{first_part}")
            pieces = []
            for q0, q1 in cuts:
                spare = len(returned) % BACK_BANKS == BACK_BANKS - 1
                back = psum.tile([P, q1 - q0, P], F32, name="back", tag="single" if spare else "sums", bufs=1 if spare else 3)
                returned.append(back)
                for q in range(q0, q1):
                    nc.scalar.activation(scaled[:, q, :], there[:, q - first_part, :], ACT.Copy, scale=gate2_by_token[:, q : q + 1])
                    nc.tensor.transpose(back[:, q - q0, :], scaled[:, q, :], ident[:])
                pieces.append((q0 * P, q1 * P, back[:].rearrange("p q t -> p (q t)")))
            return pieces

        backs = {}
        last = shared[-1]
        there = fetch_and_turn(shared[0], 0, PARTS)
        for b in shared[:-1]:
            ahead = fetch_and_turn(b + 1, 0, PARTS if b + 1 < last else PARTS // 2)
            backs[b] = scale_and_return(b, there, [(0, PARTS)])
            there = ahead
        ahead = fetch_and_turn(last, PARTS // 2, PARTS)
        backs[last] = scale_and_return(last, there, LAST_CUTS[:1]) + scale_and_return(last, ahead, LAST_CUTS[1:])

        alone = BLOCKS - 1
        firsts = {0: gated(0, 0, pos1_sb, None)}
        second = gated(0, 1, pos2_sb, None)
        firsts[1] = gated(1, 0, pos1_sb, None)
        add_and_store(0, firsts[0], [(0, T, second[:])])
        for b in list(range(2, LAG + 1)) + [alone]:
            firsts[b] = gated(b, 0, pos1_sb, None)
        add_and_store(1, firsts[1], backs[1])
        second = gated(alone, 1, pos2_sb, 1)
        add_and_store(2, firsts[2], backs[2])
        add_and_store(alone, firsts[alone], [(0, T, second[:])])
        for b in range(LAG + 1, alone):
            firsts[b] = gated(b, 0, pos1_sb, b - LAG + 1, 0, T if b < last else T // 2)
            add_and_store(b - LAG + 2, firsts[b - LAG + 2], backs[b - LAG + 2])
        add_and_store(last - 1, firsts[last - 1], backs[last - 1])
        other_half = gated(last, 0, pos1_sb, last - 1, T // 2, T)
        add_and_store(last, firsts[last], backs[last][:1])
        add_and_store(last, other_half, backs[last][1:], T // 2)
